import numpy as np
import ml_dtypes


def mxq(x, axis, fmt="e4m3"):
    dtype, down = {"e4m3": (ml_dtypes.float8_e4m3fn, 7), "e5m2": (ml_dtypes.float8_e5m2, 14)}[fmt]
    v = np.moveaxis(np.asarray(x, np.float32).astype(ml_dtypes.bfloat16).astype(np.float64), axis, -1)
    blocks = v.reshape(v.shape[:-1] + (-1, 32))
    amax = np.abs(blocks).max(-1, keepdims=True)
    byte = np.maximum(np.where(amax > 0, np.frexp(amax)[1] - 1 + 127, 0) - down, 1)
    scale = np.exp2(byte - 127.0)
    codes = (blocks / scale).astype(np.float32).astype(dtype).astype(np.float64)
    return np.moveaxis((codes * scale).reshape(v.shape), -1, axis)


WIDE = False


def mx_kscale(k):
    if not WIDE:
        return np.ones(k)
    levels = np.array([18, -18])
    if k % 512:
        return np.exp2(np.random.permutation(np.resize(levels, k // 32))).repeat(32)
    a = np.empty((k // 512, 16))
    for p in range(k // 512):
        a[p, :8] = np.random.permutation(np.resize(levels, 8))
        for g in range(8):
            far = levels[np.abs(levels - a[p, g]) >= 10]
            a[p, g + 8] = far[np.random.randint(len(far))]
    return np.exp2(a.ravel()).repeat(32)


def f64(x):
    return np.asarray(x).astype(np.float64)


def striped(idx):
    return np.tile(np.asarray(idx).reshape(-1, 16).T, (8, 1)).astype(np.uint16)


def unstriped(offs):
    return offs[:16].T.reshape(-1).astype(np.int64)


B, N, T, D, R = 1, 512, 2048, 512, 1024


def setup_inputs():
    n = np.random.standard_normal
    idx = np.random.permutation(T)[:B * N]
    s = mx_kscale(D)[:, None]
    u = np.ones(T)
    u[idx] = mx_kscale(B * N)
    r = np.random.uniform(0.5, 2.0, T) * u
    x = n((B, D, R))
    return {
        "xT": (x * s).astype(np.float32),
        "wT": (n((D, T)) * (1.00 / np.sqrt(D)) / s / r).astype(np.float32),
        "y": np.random.randint(0, 2, (B, R, N)).astype(np.float32),
        "wt": (np.random.uniform(0.5, 1.5, (B, R, 1)) * 1.0 / np.sqrt(R)).astype(np.float32),
        "ts": np.tile(r, (128, 1)).astype(np.float32),
        "offs": striped(idx),
    }


def reference(xT, wT, y, wt, ts, offs):
    idx = unstriped(offs)
    pick = lambda x: x[:, idx].reshape(x.shape[0], B, N).transpose(1, 0, 2)
    w = pick(f64(wT))
    a = mxq(f64(xT), 1, "e4m3").transpose(0, 2, 1) @ mxq(w, 1, "e4m3")
    ts_ = pick(f64(ts))[:, :1, :]
    a = a * ts_
    g = f64(wt) * (1.0 / (1.0 + np.exp(-a)) - f64(y))
    g = g * ts_
    gx = mxq(g, 2, "e5m2") @ mxq(w, 2, "e4m3").transpose(0, 2, 1)
    return gx

@@ -1,0 +1,282 @@
+from contextlib import ExitStack
+
+import concourse.mybir as mybir
+from concourse.masks import make_identity
+
+N, T, D, R = 512, 2048, 512, 1024
+P = 128
+PACK = 4
+BLOCK = 128
+CHUNK = 256
+FLOPS = 2 * 2 * R * N * D
+BYTES = 4 * (D * R + D * T + R * N + R + T + R * D) + 2 * P * (N // 16)
+
+F32 = mybir.dt.float32
+BF16 = mybir.dt.bfloat16
+U32 = mybir.dt.uint32
+U16 = mybir.dt.uint16
+U8 = mybir.dt.uint8
+E4M3 = mybir.dt.float8_e4m3fn_x4
+E5M2 = mybir.dt.float8_e5m2_x4
+ACT = mybir.ActivationFunctionType
+ALU = mybir.AluOpType
+
+
+def tile_attend_gnce_x_ts_kernel(tc, xT, wT, y, wt, ts, offs, out):
+    nc = tc.nc
+    n_chunks = R // CHUNK
+    n_blocks = R // BLOCK
+    per_chunk = CHUNK // BLOCK
+
+    with ExitStack() as ctx:
+        keep = ctx.enter_context(tc.tile_pool(name="keep", bufs=1))
+        psum = ctx.enter_context(tc.psum_pool(name="psum", bufs=1))
+
+        def sbuf(name, shape, dtype):
+            return keep.tile(shape, dtype, name=name, align_bytes=64)
+
+        def bank(k):
+            return psum.tile([P, 512], F32, name="bank%d" % k)
+
+        offsets = keep.tile([P, N // 16], U16, name="offsets")
+        nc.sync.dma_start(offsets[:], offs)
+        wt_rows = sbuf("wt_rows", [P, 8], F32)
+        nc.sync.dma_start(wt_rows[:], wt[0].rearrange("(p c) o -> p (c o)", c=8))
+        ts_table = sbuf("ts_table", [P, T], F32)
+        nc.vector.memset(ts_table[:], 0.0)
+        nc.scalar.dma_start(ts_table[0:1, :], ts[0:1, :])
+
+        w_view = wT.rearrange("(p j) t -> p j t", j=PACK)
+        w_planes = []
+        for j in range(PACK):
+            plane = sbuf("w_plane%d" % j, [P, T], F32)
+            nc.sync.dma_start(plane[:], w_view[:, j, :])
+            w_planes.append(plane)
+
+        x_view = xT[0].rearrange("(p j) r -> p j r", j=PACK)
+        x_tiles = {}
+        y_tiles = {}
+
+        def load_x(first, count):
+            tile = sbuf("x_raw%d" % first, [P, PACK, count * CHUNK], F32)
+            nc.sync.dma_start(tile[:], x_view[:, :, first * CHUNK : (first + count) * CHUNK])
+            for k in range(count):
+                x_tiles[first + k] = tile[:, :, k * CHUNK : (k + 1) * CHUNK]
+
+        def load_y(k):
+            tile = sbuf("y_raw%d" % k, [P, per_chunk, N], F32)
+            nc.sync.dma_start(tile[:], y[0][k * CHUNK : (k + 1) * CHUNK, :].rearrange("(c p) i -> p c i", p=P))
+            for c in range(per_chunk):
+                y_tiles[k * per_chunk + c] = tile[:, c, :]
+
+        load_x(0, 1)
+        load_y(0)
+        load_x(1, 1)
+        load_y(1)
+        load_x(2, 1)
+        load_x(3, 1)
+        load_y(2)
+        load_y(3)
+
+        ident = sbuf("ident", [P, P], F32)
+        make_identity(nc, ident[:])
+        warm = sbuf("warm", [P, 1], F32)
+        nc.scalar.activation(warm[:], wt_rows[:, 0:1], ACT.Sigmoid)
+
+        factor = sbuf("factor", [P, PACK, R], F32)
+        wt_wide = sbuf("wt_wide", [P, R], F32)
+        for h in range(2):
+            wt_bank = bank(1 + h)
+            for c in range(4):
+                col = 4 * h + c
+                nc.tensor.transpose(
+                    wt_bank[:, c * P : (c + 1) * P], wt_rows[:, col : col + 1].to_broadcast([P, P]), ident[:]
+                )
+            nc.scalar.copy(
+                wt_wide[:].rearrange("m (p h c) -> m h p c", h=2, c=4)[:, h],
+                wt_bank[:].rearrange("m (c p) -> m p c", c=4),
+            )
+
+        ts_listed = sbuf("ts_listed", [P, N], F32)
+        nc.vector.tensor_copy(ts_listed[:], ts_table[:].indirect(offsets[:]))
+        ts_bank = bank(0)
+        for t in range(PACK):
+            nc.tensor.transpose(ts_bank[:, t * P : (t + 1) * P], ts_listed[:, t::PACK], ident[:])
+        ts_slot = sbuf("ts_slot", [P, PACK], F32)
+        nc.scalar.copy(ts_slot[:], ts_bank[:, 0::P])
+
+        def factor_on_scalar(t):
+            nc.scalar.activation(factor[:, t, :], wt_wide[:], ACT.Copy, scale=ts_slot[:, t : t + 1])
+
+        def factor_on_vector(t):
+            nc.vector.tensor_scalar(factor[:, t, :], wt_wide[:], ts_slot[:, t : t + 1], None, ALU.mult)
+
+        w_listed = sbuf("w_listed", [P, PACK, N], F32)
+        w2_codes = sbuf("w2_codes", [P, D], U32)
+        w2_scales = sbuf("w2_scales", [P, D], U8)
+        w2_in = {}
+
+        def gather_w(j):
+            nc.vector.tensor_copy(w_listed[:, j, :], w_planes[j][:].indirect(offsets[:]))
+
+        def turn_w(j):
+            turned = bank(6 + j % 2)
+            for t in range(PACK):
+                nc.tensor.transpose(turned[:, t * P : (t + 1) * P], w_listed[:, j, t::PACK], ident[:])
+            w2_in[j] = sbuf("w2_in%d" % j, [P, P * PACK], BF16)
+            nc.scalar.copy(
+                w2_in[j][:].rearrange("m (p t) -> m p t", t=PACK), turned[:].rearrange("m (t p) -> m p t", t=PACK)
+            )
+
+        def quantise_w2(j):
+            nc.vector.quantize_mx(
+                w2_codes[:, j * P : (j + 1) * P].bitcast(E4M3), w2_scales[:, j * P : (j + 1) * P], w2_in[j][:]
+            )
+
+        gather_w(0)
+        gather_w(1)
+        factor_on_scalar(0)
+        turn_w(0)
+        factor_on_scalar(1)
+        turn_w(1)
+        factor_on_vector(2)
+        gather_w(2)
+        turn_w(2)
+        factor_on_vector(3)
+        quantise_w2(0)
+        quantise_w2(1)
+        gather_w(3)
+
+        w1_in = sbuf("w1_in", [P, N * PACK], BF16)
+        nc.vector.tensor_copy(
+            w1_in[:].rearrange("p (t m j) -> p m j t", t=PACK, j=PACK),
+            w_listed[:].rearrange("p j (m t) -> p m j t", t=PACK),
+        )
+
+        x_in = {}
+        x_codes = {}
+        x_scales = {}
+
+        def group_x(k, engine_copy):
+            x_in[k] = sbuf("x_in%d" % k, [P, CHUNK * PACK], BF16)
+            engine_copy(
+                x_in[k][:].rearrange("p (c i j) -> p c j i", i=4, j=PACK),
+                x_tiles[k].rearrange("p j (c i) -> p c j i", i=4),
+            )
+
+        def quantise_x(k):
+            x_codes[k] = sbuf("x_codes%d" % k, [P, CHUNK], U32)
+            x_scales[k] = sbuf("x_scales%d" % k, [P, CHUNK], U8)
+            nc.vector.quantize_mx(x_codes[k][:].bitcast(E4M3), x_scales[k][:], x_in[k][:])
+
+        group_x(0, nc.scalar.copy)
+        turn_w(3)
+        quantise_x(0)
+        w1_codes = []
+        w1_scales = []
+        for half in range(2):
+            w1_codes.append(sbuf("w1_codes%d" % half, [P, 2 * P], U32))
+            w1_scales.append(sbuf("w1_scales%d" % half, [P, 2 * P], U8))
+            nc.vector.quantize_mx(
+                w1_codes[half][:].bitcast(E4M3),
+                w1_scales[half][:],
+                w1_in[:, half * 2 * P * PACK : (half + 1) * 2 * P * PACK],
+            )
+
+        sig = {}
+        diff = {}
+        h_in = {}
+        h_codes = {}
+        h_scales = {}
+        y_banks = {}
+
+        def scores(k, half):
+            if half == 0:
+                sig[k] = sbuf("sig%d" % k, [P, PACK, CHUNK], F32)
+            acc = bank((2 * k + half) % 3)
+            for u in range(2):
+                nc.tensor.matmul_mx(
+                    acc[:, u * CHUNK : (u + 1) * CHUNK],
+                    lhsT=w1_codes[half][:, u * P : (u + 1) * P].bitcast(E4M3),
+                    lhsT_scale=w1_scales[half][:, u * P : (u + 1) * P],
+                    rhs=x_codes[k][:].bitcast(E4M3),
+                    rhs_scale=x_scales[k][:],
+                    start=True,
+                    stop=True,
+                )
+            for u in range(2):
+                t = 2 * half + u
+                nc.scalar.activation(
+                    sig[k][:, t, :], acc[:, u * CHUNK : (u + 1) * CHUNK], ACT.Sigmoid, scale=ts_slot[:, t : t + 1]
+                )
+
+        def turn_y(b):
+            y_banks[b] = bank(3 + b % 3)
+            for t in range(PACK):
+                nc.tensor.transpose(y_banks[b][:, t * P : (t + 1) * P], y_tiles[b][:, t::PACK], ident[:])
+
+        def subtract(b):
+            k, c = divmod(b, per_chunk)
+            diff[b] = sbuf("diff%d" % b, [P, PACK, BLOCK], F32)
+            nc.vector.tensor_tensor(
+                diff[b][:],
+                sig[k][:, :, c * BLOCK : (c + 1) * BLOCK],
+                y_banks[b][:].rearrange("m (t r) -> m t r", t=PACK),
+                ALU.subtract,
+            )
+
+        def weigh(b):
+            h_in[b] = sbuf("h_in%d" % b, [P, BLOCK * PACK], BF16)
+            nc.vector.tensor_tensor(
+                h_in[b][:].rearrange("m (c i t) -> m c t i", i=4, t=PACK),
+                diff[b][:].rearrange("m t (c i) -> m c t i", i=4),
+                factor[:, :, b * BLOCK : (b + 1) * BLOCK].rearrange("m t (c i) -> m c t i", i=4),
+                ALU.mult,
+            )
+
+        def quantise_h(b):
+            h_codes[b] = sbuf("h_codes%d" % b, [P, BLOCK], U32)
+            h_scales[b] = sbuf("h_scales%d" % b, [P, BLOCK], U8)
+            nc.vector.quantize_mx(h_codes[b][:].bitcast(E5M2), h_scales[b][:], h_in[b][:])
+
+        def gradient(b):
+            acc = bank(6 + b % 2)
+            nc.tensor.matmul_mx(
+                acc[:],
+                lhsT=h_codes[b][:].bitcast(E5M2),
+                lhsT_scale=h_scales[b][:],
+                rhs=w2_codes[:].bitcast(E4M3),
+                rhs_scale=w2_scales[:],
+                start=True,
+                stop=True,
+            )
+            result = sbuf("result%d" % b, [P, D], F32)
+            nc.scalar.copy(
+                result[:].rearrange("r (p j) -> r p j", j=PACK), acc[:].rearrange("r (j p) -> r p j", j=PACK)
+            )
+            nc.sync.dma_start(out[0][b * BLOCK : (b + 1) * BLOCK, :], result[:])
+
+        turn_y(0)
+        scores(0, 0)
+        scores(0, 1)
+        group_x(1, nc.vector.tensor_copy)
+        quantise_w2(2)
+        quantise_w2(3)
+        quantise_x(1)
+        for b in range(n_blocks + 2):
+            k, c = divmod(b, per_chunk)
+            if c == 0 and 2 <= k + 1 < n_chunks:
+                quantise_x(k + 1)
+            if b + 1 < n_blocks:
+                turn_y(b + 1)
+            if k + 1 < n_chunks:
+                scores(k + 1, c)
+            if b < n_blocks:
+                subtract(b)
+            if c == 1 and k + 2 < n_chunks:
+                group_x(k + 2, nc.scalar.copy)
+            if 1 <= b <= n_blocks:
+                weigh(b - 1)
+            if b >= 2:
+                quantise_h(b - 2)
+                gradient(b - 2)

@@ -24,24 +24,23 @@ ALU = mybir.AluOpType
 
 def tile_attend_gnce_x_ts_kernel(tc, xT, wT, y, wt, ts, offs, out):
     nc = tc.nc
-    n_chunks = R // CHUNK
     n_blocks = R // BLOCK
-    per_chunk = CHUNK // BLOCK
 
     with ExitStack() as ctx:
         keep = ctx.enter_context(tc.tile_pool(name="keep", bufs=1))
+        stage = ctx.enter_context(tc.tile_pool(name="stage", bufs=PACK))
         psum = ctx.enter_context(tc.psum_pool(name="psum", bufs=1))
 
         def sbuf(name, shape, dtype):
             return keep.tile(shape, dtype, name=name, align_bytes=64)
 
-        def bank(k):
-            return psum.tile([P, 512], F32, name="bank%d" % k)
+        def bank(k, dtype=F32):
+            return psum.tile([P, 512], dtype, name="bank%d" % k)
 
         offsets = keep.tile([P, N // 16], U16, name="offsets")
         nc.sync.dma_start(offsets[:], offs)
         wt_rows = sbuf("wt_rows", [P, 8], F32)
-        nc.sync.dma_start(wt_rows[:], wt[0].rearrange("(p c) o -> p (c o)", c=8))
+        nc.scalar.dma_start(wt_rows[:], wt[0].rearrange("(p c) o -> p (c o)", c=8))
         ts_table = sbuf("ts_table", [P, T], F32)
         nc.vector.memset(ts_table[:], 0.0)
         nc.scalar.dma_start(ts_table[0:1, :], ts[0:1, :])
@@ -49,44 +48,21 @@ def tile_attend_gnce_x_ts_kernel(tc, xT, wT, y, wt, ts, offs, out):
         w_view = wT.rearrange("(p j) t -> p j t", j=PACK)
         w_planes = []
         for j in range(PACK):
-            plane = sbuf("w_plane%d" % j, [P, T], F32)
+            plane = stage.tile([P, T], F32, name="staged")
             nc.sync.dma_start(plane[:], w_view[:, j, :])
             w_planes.append(plane)
 
-        x_view = xT[0].rearrange("(p j) r -> p j r", j=PACK)
-        x_tiles = {}
-        y_tiles = {}
-
-        def load_x(first, count):
-            tile = sbuf("x_raw%d" % first, [P, PACK, count * CHUNK], F32)
-            nc.sync.dma_start(tile[:], x_view[:, :, first * CHUNK : (first + count) * CHUNK])
-            for k in range(count):
-                x_tiles[first + k] = tile[:, :, k * CHUNK : (k + 1) * CHUNK]
-
-        def load_y(k):
-            tile = sbuf("y_raw%d" % k, [P, per_chunk, N], F32)
-            nc.sync.dma_start(tile[:], y[0][k * CHUNK : (k + 1) * CHUNK, :].rearrange("(c p) i -> p c i", p=P))
-            for c in range(per_chunk):
-                y_tiles[k * per_chunk + c] = tile[:, c, :]
-
-        load_x(0, 1)
-        load_y(0)
-        load_x(1, 1)
-        load_y(1)
-        load_x(2, 1)
-        load_x(3, 1)
-        load_y(2)
-        load_y(3)
-
         ident = sbuf("ident", [P, P], F32)
         make_identity(nc, ident[:])
+        ident_bf = sbuf("ident_bf", [P, P], BF16)
+        make_identity(nc, ident_bf[:])
         warm = sbuf("warm", [P, 1], F32)
         nc.scalar.activation(warm[:], wt_rows[:, 0:1], ACT.Sigmoid)
 
         factor = sbuf("factor", [P, PACK, R], F32)
         wt_wide = sbuf("wt_wide", [P, R], F32)
         for h in range(2):
-            wt_bank = bank(1 + h)
+            wt_bank = bank(2 + h)
             for c in range(4):
                 col = 4 * h + c
                 nc.tensor.transpose(
@@ -99,7 +75,7 @@ def tile_attend_gnce_x_ts_kernel(tc, xT, wT, y, wt, ts, offs, out):
 
         ts_listed = sbuf("ts_listed", [P, N], F32)
         nc.vector.tensor_copy(ts_listed[:], ts_table[:].indirect(offsets[:]))
-        ts_bank = bank(0)
+        ts_bank = bank(4)
         for t in range(PACK):
             nc.tensor.transpose(ts_bank[:, t * P : (t + 1) * P], ts_listed[:, t::PACK], ident[:])
         ts_slot = sbuf("ts_slot", [P, PACK], F32)
@@ -111,21 +87,29 @@ def tile_attend_gnce_x_ts_kernel(tc, xT, wT, y, wt, ts, offs, out):
         def factor_on_vector(t):
             nc.vector.tensor_scalar(factor[:, t, :], wt_wide[:], ts_slot[:, t : t + 1], None, ALU.mult)
 
-        w_listed = sbuf("w_listed", [P, PACK, N], F32)
+        w1_in = sbuf("w1_in", [P, N * PACK], BF16)
         w2_codes = sbuf("w2_codes", [P, D], U32)
         w2_scales = sbuf("w2_scales", [P, D], U8)
         w2_in = {}
+        w2_banks = {}
 
         def gather_w(j):
-            nc.vector.tensor_copy(w_listed[:, j, :], w_planes[j][:].indirect(offsets[:]))
+            nc.vector.tensor_copy(
+                w1_in[:].rearrange("p (t m j) -> p j m t", t=PACK, j=PACK)[:, j],
+                w_planes[j][:].indirect(offsets[:]),
+            )
 
         def turn_w(j):
-            turned = bank(6 + j % 2)
+            turned = bank(6 + j % 2, BF16)
+            plane = w1_in[:].rearrange("p (t m j) -> p j t m", t=PACK, j=PACK)[:, j]
             for t in range(PACK):
-                nc.tensor.transpose(turned[:, t * P : (t + 1) * P], w_listed[:, j, t::PACK], ident[:])
+                nc.tensor.transpose(turned[:, t * P : (t + 1) * P], plane[:, t], ident_bf[:])
+            w2_banks[j] = turned
+
+        def group_w2(j):
             w2_in[j] = sbuf("w2_in%d" % j, [P, P * PACK], BF16)
             nc.scalar.copy(
-                w2_in[j][:].rearrange("m (p t) -> m p t", t=PACK), turned[:].rearrange("m (t p) -> m p t", t=PACK)
+                w2_in[j][:].rearrange("m (p t) -> m p t", t=PACK), w2_banks[j][:].rearrange("m (t p) -> m p t", t=PACK)
             )
 
         def quantise_w2(j):
@@ -134,53 +118,76 @@ def tile_attend_gnce_x_ts_kernel(tc, xT, wT, y, wt, ts, offs, out):
             )
 
         gather_w(0)
-        gather_w(1)
-        factor_on_scalar(0)
         turn_w(0)
-        factor_on_scalar(1)
+        group_w2(0)
+        factor_on_scalar(0)
+        gather_w(1)
         turn_w(1)
-        factor_on_vector(2)
+        group_w2(1)
+        factor_on_scalar(1)
         gather_w(2)
         turn_w(2)
-        factor_on_vector(3)
-        quantise_w2(0)
-        quantise_w2(1)
+        group_w2(2)
         gather_w(3)
+        turn_w(3)
 
-        w1_in = sbuf("w1_in", [P, N * PACK], BF16)
-        nc.vector.tensor_copy(
-            w1_in[:].rearrange("p (t m j) -> p m j t", t=PACK, j=PACK),
-            w_listed[:].rearrange("p j (m t) -> p m j t", t=PACK),
-        )
+        x_view = xT[0].rearrange("(p j) r -> p j r", j=PACK)
+        x_tiles = {}
+        y_tiles = {}
+        x_pairs = {}
+        y_pairs = {}
 
+        def load_x(k):
+            if k % 2 == 0:
+                x_pairs[k // 2] = stage.tile([P, 2, PACK, CHUNK], F32, name="staged")
+            x_tiles[k] = x_pairs[k // 2][:, k % 2]
+            nc.sync.dma_start(x_tiles[k], x_view[:, :, k * CHUNK : (k + 1) * CHUNK])
+
+        def load_y(k):
+            if k % 2 == 0:
+                y_pairs[k // 2] = stage.tile([P, 2, 2, N], F32, name="staged")
+            half = y_pairs[k // 2][:, k % 2]
+            nc.sync.dma_start(half, y[0][k * CHUNK : (k + 1) * CHUNK, :].rearrange("(c p) i -> p c i", p=P))
+            for c in range(2):
+                y_tiles[2 * k + c] = half[:, c, :]
+
+        load_x(0)
+        load_x(1)
+        load_y(0)
+        load_x(2)
+        load_y(1)
+        load_x(3)
+        load_y(2)
+        load_y(3)
+
+        units = [(0, BLOCK), (BLOCK, BLOCK), (CHUNK, CHUNK), (2 * CHUNK, CHUNK), (3 * CHUNK, CHUNK)]
         x_in = {}
         x_codes = {}
         x_scales = {}
 
-        def group_x(k, engine_copy):
-            x_in[k] = sbuf("x_in%d" % k, [P, CHUNK * PACK], BF16)
+        def group_x(u, engine_copy):
+            first, rows = units[u]
+            k, skip = divmod(first, CHUNK)
+            x_in[u] = sbuf("x_in%d" % u, [P, rows * PACK], BF16)
             engine_copy(
-                x_in[k][:].rearrange("p (c i j) -> p c j i", i=4, j=PACK),
-                x_tiles[k].rearrange("p j (c i) -> p c j i", i=4),
+                x_in[u][:].rearrange("p (c i j) -> p c j i", i=2, j=PACK),
+                x_tiles[k][:, :, skip : skip + rows].rearrange("p j (c i) -> p c j i", i=2),
             )
 
-        def quantise_x(k):
-            x_codes[k] = sbuf("x_codes%d" % k, [P, CHUNK], U32)
-            x_scales[k] = sbuf("x_scales%d" % k, [P, CHUNK], U8)
-            nc.vector.quantize_mx(x_codes[k][:].bitcast(E4M3), x_scales[k][:], x_in[k][:])
+        def quantise_x(u):
+            rows = units[u][1]
+            x_codes[u] = sbuf("x_codes%d" % u, [P, rows], U32)
+            x_scales[u] = sbuf("x_scales%d" % u, [P, rows], U8)
+            nc.vector.quantize_mx(x_codes[u][:].bitcast(E4M3), x_scales[u][:], x_in[u][:])
 
-        group_x(0, nc.scalar.copy)
-        turn_w(3)
-        quantise_x(0)
-        w1_codes = []
-        w1_scales = []
-        for half in range(2):
-            w1_codes.append(sbuf("w1_codes%d" % half, [P, 2 * P], U32))
-            w1_scales.append(sbuf("w1_scales%d" % half, [P, 2 * P], U8))
+        w1_codes = {}
+        w1_scales = {}
+
+        def quantise_w1(t):
+            w1_codes[t] = sbuf("w1_codes%d" % t, [P, P], U32)
+            w1_scales[t] = sbuf("w1_scales%d" % t, [P, P], U8)
             nc.vector.quantize_mx(
-                w1_codes[half][:].bitcast(E4M3),
-                w1_scales[half][:],
-                w1_in[:, half * 2 * P * PACK : (half + 1) * 2 * P * PACK],
+                w1_codes[t][:].bitcast(E4M3), w1_scales[t][:], w1_in[:, t * P * PACK : (t + 1) * P * PACK]
             )
 
         sig = {}
@@ -188,58 +195,36 @@ def tile_attend_gnce_x_ts_kernel(tc, xT, wT, y, wt, ts, offs, out):
         h_in = {}
         h_codes = {}
         h_scales = {}
-        y_banks = {}
 
-        def scores(k, half):
-            if half == 0:
-                sig[k] = sbuf("sig%d" % k, [P, PACK, CHUNK], F32)
-            acc = bank((2 * k + half) % 3)
-            for u in range(2):
+        def scores(u, places, k):
+            first, rows = units[u]
+            if places[0] == 0:
+                tile = sbuf("sig%d" % u, [P, PACK, rows], F32)
+                for c in range(rows // BLOCK):
+                    sig[first // BLOCK + c] = tile[:, :, c * BLOCK : (c + 1) * BLOCK]
+                sig["unit", u] = tile
+            acc = bank(k)
+            for n, t in enumerate(places):
                 nc.tensor.matmul_mx(
-                    acc[:, u * CHUNK : (u + 1) * CHUNK],
-                    lhsT=w1_codes[half][:, u * P : (u + 1) * P].bitcast(E4M3),
-                    lhsT_scale=w1_scales[half][:, u * P : (u + 1) * P],
-                    rhs=x_codes[k][:].bitcast(E4M3),
-                    rhs_scale=x_scales[k][:],
+                    acc[:, n * rows : (n + 1) * rows],
+                    lhsT=w1_codes[t][:].bitcast(E4M3),
+                    lhsT_scale=w1_scales[t][:],
+                    rhs=x_codes[u][:].bitcast(E4M3),
+                    rhs_scale=x_scales[u][:],
                     start=True,
                     stop=True,
                 )
-            for u in range(2):
-                t = 2 * half + u
+            for n, t in enumerate(places):
                 nc.scalar.activation(
-                    sig[k][:, t, :], acc[:, u * CHUNK : (u + 1) * CHUNK], ACT.Sigmoid, scale=ts_slot[:, t : t + 1]
+                    sig["unit", u][:, t, :], acc[:, n * rows : (n + 1) * rows], ACT.Sigmoid, scale=ts_slot[:, t : t + 1]
                 )
-
-        def turn_y(b):
-            y_banks[b] = bank(3 + b % 3)
-            for t in range(PACK):
-                nc.tensor.transpose(y_banks[b][:, t * P : (t + 1) * P], y_tiles[b][:, t::PACK], ident[:])
-
-        def subtract(b):
-            k, c = divmod(b, per_chunk)
-            diff[b] = sbuf("diff%d" % b, [P, PACK, BLOCK], F32)
-            nc.vector.tensor_tensor(
-                diff[b][:],
-                sig[k][:, :, c * BLOCK : (c + 1) * BLOCK],
-                y_banks[b][:].rearrange("m (t r) -> m t r", t=PACK),
-                ALU.subtract,
-            )
-
-        def weigh(b):
-            h_in[b] = sbuf("h_in%d" % b, [P, BLOCK * PACK], BF16)
-            nc.vector.tensor_tensor(
-                h_in[b][:].rearrange("m (c i t) -> m c t i", i=4, t=PACK),
-                diff[b][:].rearrange("m t (c i) -> m c t i", i=4),
-                factor[:, :, b * BLOCK : (b + 1) * BLOCK].rearrange("m t (c i) -> m c t i", i=4),
-                ALU.mult,
-            )
 
         def quantise_h(b):
             h_codes[b] = sbuf("h_codes%d" % b, [P, BLOCK], U32)
             h_scales[b] = sbuf("h_scales%d" % b, [P, BLOCK], U8)
             nc.vector.quantize_mx(h_codes[b][:].bitcast(E5M2), h_scales[b][:], h_in[b][:])
 
-        def gradient(b):
+        def gradient(b, engine_copy):
             acc = bank(6 + b % 2)
             nc.tensor.matmul_mx(
                 acc[:],
@@ -251,32 +236,87 @@ def tile_attend_gnce_x_ts_kernel(tc, xT, wT, y, wt, ts, offs, out):
                 stop=True,
             )
             result = sbuf("result%d" % b, [P, D], F32)
-            nc.scalar.copy(
+            engine_copy(
                 result[:].rearrange("r (p j) -> r p j", j=PACK), acc[:].rearrange("r (j p) -> r p j", j=PACK)
             )
             nc.sync.dma_start(out[0][b * BLOCK : (b + 1) * BLOCK, :], result[:])
 
-        turn_y(0)
-        scores(0, 0)
-        scores(0, 1)
-        group_x(1, nc.vector.tensor_copy)
-        quantise_w2(2)
-        quantise_w2(3)
+        group_x(0, nc.scalar.copy)
+        group_x(1, nc.scalar.copy)
+        group_x(2, nc.scalar.copy)
+        quantise_w1(0)
+        quantise_w1(1)
+        quantise_x(0)
+        quantise_w1(2)
+        quantise_w1(3)
         quantise_x(1)
-        for b in range(n_blocks + 2):
-            k, c = divmod(b, per_chunk)
-            if c == 0 and 2 <= k + 1 < n_chunks:
-                quantise_x(k + 1)
-            if b + 1 < n_blocks:
-                turn_y(b + 1)
-            if k + 1 < n_chunks:
-                scores(k + 1, c)
-            if b < n_blocks:
-                subtract(b)
-            if c == 1 and k + 2 < n_chunks:
-                group_x(k + 2, nc.scalar.copy)
-            if 1 <= b <= n_blocks:
-                weigh(b - 1)
-            if b >= 2:
-                quantise_h(b - 2)
-                gradient(b - 2)
+
+        sig_banks = {}
+        diff_banks = {}
+
+        def turn_sig(b):
+            sig_banks[b] = bank(2 + b % 2)
+            for t in range(PACK):
+                nc.tensor.transpose(sig_banks[b][:, t * P : (t + 1) * P], sig[b][:, t, :], ident[:])
+
+        def subtract(b):
+            diff[b] = sbuf("diff%d" % b, [P, PACK, P], F32)
+            nc.vector.tensor_tensor(
+                diff[b][:].rearrange("r t (c i) -> r c t i", i=2),
+                sig_banks[b][:].rearrange("r (t c i) -> r c t i", t=PACK, i=2),
+                y_tiles[b].rearrange("r (c i t) -> r c t i", t=PACK, i=2),
+                ALU.subtract,
+            )
+
+        def turn_diff(b):
+            diff_banks[b] = bank(4 + b % 2)
+            for t in range(PACK):
+                nc.tensor.transpose(diff_banks[b][:, t * P : (t + 1) * P], diff[b][:, t, :], ident[:])
+
+        def weigh(b):
+            h_in[b] = sbuf("h_in%d" % b, [P, BLOCK * PACK], BF16)
+            nc.vector.tensor_tensor(
+                h_in[b][:].rearrange("m (c i t) -> m c t i", i=2, t=PACK),
+                diff_banks[b][:].rearrange("m (t c i) -> m c t i", t=PACK, i=2),
+                factor[:, :, b * BLOCK : (b + 1) * BLOCK].rearrange("m t (c i) -> m c t i", i=2),
+                ALU.mult,
+            )
+
+        scores(0, [0, 1, 2, 3], 0)
+        scores(1, [0, 1, 2, 3], 1)
+        factor_on_vector(2)
+        factor_on_vector(3)
+        quantise_x(2)
+        for j in range(PACK - 1):
+            quantise_w2(j)
+        turn_sig(0)
+        scores(2, [0, 1], 0)
+        turn_sig(1)
+        scores(2, [2, 3], 1)
+        group_w2(3)
+        group_x(3, nc.vector.tensor_copy)
+        for s in range(-2, n_blocks + 2):
+            if 0 <= s + 1 < n_blocks:
+                turn_diff(s + 1)
+            if 2 <= s + 3 < n_blocks:
+                turn_sig(s + 3)
+            if s in (-1, 0):
+                scores(3, [2 * s + 2, 2 * s + 3], s + 1)
+            if s in (1, 2):
+                scores(4, [2 * s - 2, 2 * s - 1], s - 1)
+            if s >= 2:
+                gradient(s - 2, nc.vector.tensor_copy if s == n_blocks + 1 else nc.scalar.copy)
+            if s + 2 < n_blocks:
+                subtract(s + 2)
+            if s == -2:
+                quantise_x(3)
+            if s == -1:
+                quantise_w2(3)
+            if s == 0:
+                group_x(4, nc.vector.tensor_copy)
+            if 1 <= s <= n_blocks:
+                quantise_h(s - 1)
+            if 0 <= s < n_blocks:
+                weigh(s)
+            if s == 0:
+                quantise_x(4)

@@ -42,7 +42,8 @@ def tile_attend_gnce_x_ts_kernel(tc, xT, wT, y, wt, ts, offs, out):
         wt_rows = sbuf("wt_rows", [P, 8], F32)
         nc.scalar.dma_start(wt_rows[:], wt[0].rearrange("(p c) o -> p (c o)", c=8))
         ts_table = sbuf("ts_table", [P, T], F32)
-        nc.vector.memset(ts_table[:], 0.0)
+        nc.gpsimd.memset(ts_table[:, : T // 2], 0.0)
+        nc.vector.memset(ts_table[:, T // 2 :], 0.0)
         nc.scalar.dma_start(ts_table[0:1, :], ts[0:1, :])
 
         w_view = wT.rearrange("(p j) t -> p j t", j=PACK)
@@ -60,7 +61,7 @@ def tile_attend_gnce_x_ts_kernel(tc, xT, wT, y, wt, ts, offs, out):
         nc.scalar.activation(warm[:], wt_rows[:, 0:1], ACT.Sigmoid)
 
         factor = sbuf("factor", [P, PACK, R], F32)
-        wt_wide = sbuf("wt_wide", [P, R], F32)
+        wt_wide = sbuf("shared", [P, R], F32)
         for h in range(2):
             wt_bank = bank(2 + h)
             for c in range(4):
@@ -83,9 +84,6 @@ def tile_attend_gnce_x_ts_kernel(tc, xT, wT, y, wt, ts, offs, out):
 
         def factor_on_scalar(t):
             nc.scalar.activation(factor[:, t, :], wt_wide[:], ACT.Copy, scale=ts_slot[:, t : t + 1])
-
-        def factor_on_vector(t):
-            nc.vector.tensor_scalar(factor[:, t, :], wt_wide[:], ts_slot[:, t : t + 1], None, ALU.mult)
 
         w1_in = sbuf("w1_in", [P, N * PACK], BF16)
         w2_codes = sbuf("w2_codes", [P, D], U32)
@@ -125,8 +123,10 @@ def tile_attend_gnce_x_ts_kernel(tc, xT, wT, y, wt, ts, offs, out):
         turn_w(1)
         group_w2(1)
         factor_on_scalar(1)
+        factor_on_scalar(2)
         gather_w(2)
         turn_w(2)
+        factor_on_scalar(3)
         group_w2(2)
         gather_w(3)
         turn_w(3)
@@ -143,22 +143,24 @@ def tile_attend_gnce_x_ts_kernel(tc, xT, wT, y, wt, ts, offs, out):
             x_tiles[k] = x_pairs[k // 2][:, k % 2]
             nc.sync.dma_start(x_tiles[k], x_view[:, :, k * CHUNK : (k + 1) * CHUNK])
 
-        def load_y(k):
-            if k % 2 == 0:
-                y_pairs[k // 2] = stage.tile([P, 2, 2, N], F32, name="staged")
-            half = y_pairs[k // 2][:, k % 2]
-            nc.sync.dma_start(half, y[0][k * CHUNK : (k + 1) * CHUNK, :].rearrange("(c p) i -> p c i", p=P))
-            for c in range(2):
-                y_tiles[2 * k + c] = half[:, c, :]
+        def load_y(first, count):
+            if first % PACK == 0:
+                y_pairs[first // PACK] = stage.tile([P, PACK, N], F32, name="staged")
+            part = y_pairs[first // PACK][:, first % PACK : first % PACK + count, :]
+            rows = y[0][first * BLOCK : (first + count) * BLOCK, :]
+            nc.sync.dma_start(part, rows.rearrange("(c p) i -> p c i", p=P))
+            for c in range(count):
+                y_tiles[first + c] = part[:, c, :]
 
         load_x(0)
         load_x(1)
-        load_y(0)
         load_x(2)
-        load_y(1)
+        load_y(0, 1)
         load_x(3)
-        load_y(2)
-        load_y(3)
+        load_y(1, 1)
+        load_y(2, 2)
+        load_y(4, 2)
+        load_y(6, 2)
 
         units = [(0, BLOCK), (BLOCK, BLOCK), (CHUNK, CHUNK), (2 * CHUNK, CHUNK), (3 * CHUNK, CHUNK)]
         x_in = {}
@@ -168,9 +170,14 @@ def tile_attend_gnce_x_ts_kernel(tc, xT, wT, y, wt, ts, offs, out):
         def group_x(u, engine_copy):
             first, rows = units[u]
             k, skip = divmod(first, CHUNK)
-            x_in[u] = sbuf("x_in%d" % u, [P, rows * PACK], BF16)
+            if u == 0:
+                early = sbuf("shared", [P, 2 * CHUNK * PACK], BF16)
+                for v in range(3):
+                    x_in[v] = early[:, units[v][0] * PACK : (units[v][0] + units[v][1]) * PACK]
+            if u >= 3:
+                x_in[u] = sbuf("shared", [P, rows * PACK], BF16)[:]
             engine_copy(
-                x_in[u][:].rearrange("p (c i j) -> p c j i", i=2, j=PACK),
+                x_in[u].rearrange("p (c i j) -> p c j i", i=2, j=PACK),
                 x_tiles[k][:, :, skip : skip + rows].rearrange("p j (c i) -> p c j i", i=2),
             )
 
@@ -178,7 +185,7 @@ def tile_attend_gnce_x_ts_kernel(tc, xT, wT, y, wt, ts, offs, out):
             rows = units[u][1]
             x_codes[u] = sbuf("x_codes%d" % u, [P, rows], U32)
             x_scales[u] = sbuf("x_scales%d" % u, [P, rows], U8)
-            nc.vector.quantize_mx(x_codes[u][:].bitcast(E4M3), x_scales[u][:], x_in[u][:])
+            nc.vector.quantize_mx(x_codes[u][:].bitcast(E4M3), x_scales[u][:], x_in[u])
 
         w1_codes = {}
         w1_scales = {}
@@ -236,10 +243,15 @@ def tile_attend_gnce_x_ts_kernel(tc, xT, wT, y, wt, ts, offs, out):
                 stop=True,
             )
             result = sbuf("result%d" % b, [P, D], F32)
-            engine_copy(
-                result[:].rearrange("r (p j) -> r p j", j=PACK), acc[:].rearrange("r (j p) -> r p j", j=PACK)
-            )
-            nc.sync.dma_start(out[0][b * BLOCK : (b + 1) * BLOCK, :], result[:])
+            pieces = 2 if b == n_blocks - 1 else 1
+            width = P // pieces
+            for n in range(pieces):
+                cols = slice(n * width * PACK, (n + 1) * width * PACK)
+                engine_copy(
+                    result[:, cols].rearrange("r (p j) -> r p j", j=PACK),
+                    acc[:].rearrange("r (j p) -> r p j", j=PACK)[:, n * width : (n + 1) * width, :],
+                )
+                nc.sync.dma_start(out[0][b * BLOCK : (b + 1) * BLOCK, cols], result[:, cols])
 
         group_x(0, nc.scalar.copy)
         group_x(1, nc.scalar.copy)
@@ -284,35 +296,32 @@ def tile_attend_gnce_x_ts_kernel(tc, xT, wT, y, wt, ts, offs, out):
 
         scores(0, [0, 1, 2, 3], 0)
         scores(1, [0, 1, 2, 3], 1)
-        factor_on_vector(2)
-        factor_on_vector(3)
         quantise_x(2)
         for j in range(PACK - 1):
             quantise_w2(j)
+        group_x(3, nc.vector.tensor_copy)
+        quantise_x(3)
         turn_sig(0)
         scores(2, [0, 1], 0)
         turn_sig(1)
         scores(2, [2, 3], 1)
         group_w2(3)
-        group_x(3, nc.vector.tensor_copy)
         for s in range(-2, n_blocks + 2):
-            if 0 <= s + 1 < n_blocks:
-                turn_diff(s + 1)
-            if 2 <= s + 3 < n_blocks:
-                turn_sig(s + 3)
+            if s >= 2:
+                gradient(s - 2, nc.vector.tensor_copy if s == n_blocks + 1 else nc.scalar.copy)
             if s in (-1, 0):
                 scores(3, [2 * s + 2, 2 * s + 3], s + 1)
             if s in (1, 2):
                 scores(4, [2 * s - 2, 2 * s - 1], s - 1)
-            if s >= 2:
-                gradient(s - 2, nc.vector.tensor_copy if s == n_blocks + 1 else nc.scalar.copy)
+            if 0 <= s + 1 < n_blocks:
+                turn_diff(s + 1)
+            if 2 <= s + 3 < n_blocks:
+                turn_sig(s + 3)
             if s + 2 < n_blocks:
                 subtract(s + 2)
-            if s == -2:
-                quantise_x(3)
             if s == -1:
                 quantise_w2(3)
-            if s == 0:
+            if s == -1:
                 group_x(4, nc.vector.tensor_copy)
             if 1 <= s <= n_blocks:
                 quantise_h(s - 1)

@@ -39,12 +39,12 @@ def tile_attend_gnce_x_ts_kernel(tc, xT, wT, y, wt, ts, offs, out):
 
         offsets = keep.tile([P, N // 16], U16, name="offsets")
         nc.sync.dma_start(offsets[:], offs)
+        ts_rows = sbuf("ts_rows", [P, 16], F32)
+        nc.scalar.dma_start(ts_rows[:], ts[0].rearrange("(p c) -> p c", c=16))
         wt_rows = sbuf("wt_rows", [P, 8], F32)
-        nc.scalar.dma_start(wt_rows[:], wt[0].rearrange("(p c) o -> p (c o)", c=8))
-        ts_table = sbuf("ts_table", [P, T], F32)
-        nc.gpsimd.memset(ts_table[:, : T // 2], 0.0)
-        nc.vector.memset(ts_table[:, T // 2 :], 0.0)
-        nc.scalar.dma_start(ts_table[0:1, :], ts[0:1, :])
+        nc.scalar.dma_start(
+            wt_rows[:].rearrange("p (h c) -> p h c", h=2), wt[0].rearrange("(h p c) o -> p h (c o)", h=2, c=4)
+        )
 
         w_view = wT.rearrange("(p j) t -> p j t", j=PACK)
         w_planes = []
@@ -58,34 +58,48 @@ def tile_attend_gnce_x_ts_kernel(tc, xT, wT, y, wt, ts, offs, out):
         ident_bf = sbuf("ident_bf", [P, P], BF16)
         make_identity(nc, ident_bf[:])
         warm = sbuf("warm", [P, 1], F32)
-        nc.scalar.activation(warm[:], wt_rows[:, 0:1], ACT.Sigmoid)
+        nc.scalar.activation(warm[:], ts_rows[:, 0:1], ACT.Sigmoid)
 
-        factor = sbuf("factor", [P, PACK, R], F32)
-        wt_wide = sbuf("shared", [P, R], F32)
+        ts_table = sbuf("ts_table", [P, T], F32)
+        for g in range(4):
+            spread = bank(g)
+            for c in range(4):
+                col = 4 * g + c
+                nc.tensor.transpose(
+                    spread[:, c * P : (c + 1) * P], ts_rows[:, col : col + 1].to_broadcast([P, P]), ident[:]
+                )
+            copy_out = nc.scalar.copy if g % 2 == 0 else nc.vector.tensor_copy
+            copy_out(
+                ts_table[:].rearrange("m (p g c) -> m g p c", g=4, c=4)[:, g],
+                spread[:].rearrange("m (c p) -> m p c", c=4),
+            )
+
+        factor = [sbuf("factor%d" % n, [P, PACK, R // 2], F32) for n in range(2)]
+        wt_wide = [sbuf("shared", [P, R // 2], F32), sbuf("wt_late", [P, R // 2], F32)]
         for h in range(2):
-            wt_bank = bank(2 + h)
+            wt_bank = bank(4 + h)
             for c in range(4):
                 col = 4 * h + c
                 nc.tensor.transpose(
                     wt_bank[:, c * P : (c + 1) * P], wt_rows[:, col : col + 1].to_broadcast([P, P]), ident[:]
                 )
             nc.scalar.copy(
-                wt_wide[:].rearrange("m (p h c) -> m h p c", h=2, c=4)[:, h],
+                wt_wide[h][:].rearrange("m (p c) -> m p c", c=4),
                 wt_bank[:].rearrange("m (c p) -> m p c", c=4),
             )
 
         ts_listed = sbuf("ts_listed", [P, N], F32)
         nc.vector.tensor_copy(ts_listed[:], ts_table[:].indirect(offsets[:]))
-        ts_bank = bank(4)
+        ts_bank = bank(0)
         for t in range(PACK):
             nc.tensor.transpose(ts_bank[:, t * P : (t + 1) * P], ts_listed[:, t::PACK], ident[:])
         ts_slot = sbuf("ts_slot", [P, PACK], F32)
         nc.scalar.copy(ts_slot[:], ts_bank[:, 0::P])
 
-        def factor_on_scalar(t):
-            nc.scalar.activation(factor[:, t, :], wt_wide[:], ACT.Copy, scale=ts_slot[:, t : t + 1])
+        def make_factor(half, t):
+            nc.scalar.activation(factor[half][:, t, :], wt_wide[half][:], ACT.Copy, scale=ts_slot[:, t : t + 1])
 
-        w1_in = sbuf("w1_in", [P, N * PACK], BF16)
+        w1_in = sbuf("ts_table", [P, N * PACK], BF16)
         w2_codes = sbuf("w2_codes", [P, D], U32)
         w2_scales = sbuf("w2_scales", [P, D], U8)
         w2_in = {}
@@ -118,15 +132,15 @@ def tile_attend_gnce_x_ts_kernel(tc, xT, wT, y, wt, ts, offs, out):
         gather_w(0)
         turn_w(0)
         group_w2(0)
-        factor_on_scalar(0)
+        make_factor(0, 0)
         gather_w(1)
         turn_w(1)
         group_w2(1)
-        factor_on_scalar(1)
-        factor_on_scalar(2)
+        make_factor(0, 1)
+        make_factor(0, 2)
         gather_w(2)
         turn_w(2)
-        factor_on_scalar(3)
+        make_factor(0, 3)
         group_w2(2)
         gather_w(3)
         turn_w(3)
@@ -290,7 +304,7 @@ def tile_attend_gnce_x_ts_kernel(tc, xT, wT, y, wt, ts, offs, out):
             nc.vector.tensor_tensor(
                 h_in[b][:].rearrange("m (c i t) -> m c t i", i=2, t=PACK),
                 diff_banks[b][:].rearrange("m (t c i) -> m c t i", t=PACK, i=2),
-                factor[:, :, b * BLOCK : (b + 1) * BLOCK].rearrange("m t (c i) -> m c t i", i=2),
+                factor[b // 4][:, :, b % 4 * BLOCK : (b % 4 + 1) * BLOCK].rearrange("m t (c i) -> m c t i", i=2),
                 ALU.mult,
             )
 
@@ -313,6 +327,8 @@ def tile_attend_gnce_x_ts_kernel(tc, xT, wT, y, wt, ts, offs, out):
                 scores(3, [2 * s + 2, 2 * s + 3], s + 1)
             if s in (1, 2):
                 scores(4, [2 * s - 2, 2 * s - 1], s - 1)
+            if 0 <= s < PACK:
+                make_factor(1, s)
             if 0 <= s + 1 < n_blocks:
                 turn_diff(s + 1)
             if 2 <= s + 3 < n_blocks:

@@ -8,12 +8,20 @@ P = 128
 PACK = 4
 BLOCK = 128
 CHUNK = 256
+OUT_BANKS = (6, 7, 6, 7, 6, 7, 0, 1)
+SIG_LEAD = 3
+SCORE_LEAD = 5
+X4_STEP = -1
+PLANE_BYTES = 4 * T
+X_HOLD = 2
+W2_PLACE = (PACK - 1) * PLANE_BYTES
 FLOPS = 2 * 2 * R * N * D
 BYTES = 4 * (D * R + D * T + R * N + R + T + R * D) + 2 * P * (N // 16)
 
 F32 = mybir.dt.float32
 BF16 = mybir.dt.bfloat16
 U32 = mybir.dt.uint32
+I32 = mybir.dt.int32
 U16 = mybir.dt.uint16
 U8 = mybir.dt.uint8
 E4M3 = mybir.dt.float8_e4m3fn_x4
@@ -28,7 +36,7 @@ def tile_attend_gnce_x_ts_kernel(tc, xT, wT, y, wt, ts, offs, out):
 
     with ExitStack() as ctx:
         keep = ctx.enter_context(tc.tile_pool(name="keep", bufs=1))
-        stage = ctx.enter_context(tc.tile_pool(name="stage", bufs=PACK))
+        stage = ctx.enter_context(tc.tile_pool(name="stage", bufs=1))
         psum = ctx.enter_context(tc.psum_pool(name="psum", bufs=1))
 
         def sbuf(name, shape, dtype):
@@ -39,43 +47,35 @@ def tile_attend_gnce_x_ts_kernel(tc, xT, wT, y, wt, ts, offs, out):
 
         offsets = keep.tile([P, N // 16], U16, name="offsets")
         nc.sync.dma_start(offsets[:], offs)
-        ts_rows = sbuf("ts_rows", [P, 16], F32)
-        nc.scalar.dma_start(ts_rows[:], ts[0].rearrange("(p c) -> p c", c=16))
         wt_rows = sbuf("wt_rows", [P, 8], F32)
         nc.scalar.dma_start(
             wt_rows[:].rearrange("p (h c) -> p h c", h=2), wt[0].rearrange("(h p c) o -> p h (c o)", h=2, c=4)
         )
 
+        def placed(name, shape, dtype, offset):
+            return stage.tile(shape, dtype, name=name, offset=offset, align_bytes=64)
+
+        ts_table = sbuf("ts_table", [P, T], F32)
+        nc.vector.memset(ts_table[:].bitcast(I32), 0)
+        warm = placed("warm", [P, (PACK - 1) * T], F32, PLANE_BYTES)
+        nc.scalar.activation(warm[P // 2 :, 0:1], ts_table[P // 2 :, 0:1], ACT.Sigmoid)
+
         w_view = wT.rearrange("(p j) t -> p j t", j=PACK)
         w_planes = []
         for j in range(PACK):
-            plane = stage.tile([P, T], F32, name="staged")
+            plane = placed("plane%d" % j, [P, T], F32, j * PLANE_BYTES)
             nc.sync.dma_start(plane[:], w_view[:, j, :])
             w_planes.append(plane)
+            if j == 0:
+                nc.sync.dma_start(ts_table[0:1, :], ts[0:1, :])
 
         ident = sbuf("ident", [P, P], F32)
         make_identity(nc, ident[:])
         ident_bf = sbuf("ident_bf", [P, P], BF16)
         make_identity(nc, ident_bf[:])
-        warm = sbuf("warm", [P, 1], F32)
-        nc.scalar.activation(warm[:], ts_rows[:, 0:1], ACT.Sigmoid)
-
-        ts_table = sbuf("ts_table", [P, T], F32)
-        for g in range(4):
-            spread = bank(g)
-            for c in range(4):
-                col = 4 * g + c
-                nc.tensor.transpose(
-                    spread[:, c * P : (c + 1) * P], ts_rows[:, col : col + 1].to_broadcast([P, P]), ident[:]
-                )
-            copy_out = nc.scalar.copy if g % 2 == 0 else nc.vector.tensor_copy
-            copy_out(
-                ts_table[:].rearrange("m (p g c) -> m g p c", g=4, c=4)[:, g],
-                spread[:].rearrange("m (c p) -> m p c", c=4),
-            )
 
         factor = [sbuf("factor%d" % n, [P, PACK, R // 2], F32) for n in range(2)]
-        wt_wide = [sbuf("shared", [P, R // 2], F32), sbuf("wt_late", [P, R // 2], F32)]
+        wt_wide = [sbuf("wt_wide%d" % n, [P, R // 2], F32) for n in range(2)]
         for h in range(2):
             wt_bank = bank(4 + h)
             for c in range(4):
@@ -97,10 +97,13 @@ def tile_attend_gnce_x_ts_kernel(tc, xT, wT, y, wt, ts, offs, out):
         nc.scalar.copy(ts_slot[:], ts_bank[:, 0::P])
 
         def make_factor(half, t):
-            nc.scalar.activation(factor[half][:, t, :], wt_wide[half][:], ACT.Copy, scale=ts_slot[:, t : t + 1])
+            if half == 0:
+                nc.scalar.activation(factor[0][:, t, :], wt_wide[0][:], ACT.Copy, scale=ts_slot[:, t : t + 1])
+            else:
+                nc.vector.tensor_scalar(factor[1][:, t, :], wt_wide[1][:], ts_slot[:, t : t + 1], None, ALU.mult)
 
         w1_in = sbuf("ts_table", [P, N * PACK], BF16)
-        w2_codes = sbuf("w2_codes", [P, D], U32)
+        w2_codes = placed("w2_codes", [P, D], U32, W2_PLACE)
         w2_scales = sbuf("w2_scales", [P, D], U8)
         w2_in = {}
         w2_banks = {}
@@ -119,7 +122,10 @@ def tile_attend_gnce_x_ts_kernel(tc, xT, wT, y, wt, ts, offs, out):
             w2_banks[j] = turned
 
         def group_w2(j):
-            w2_in[j] = sbuf("w2_in%d" % j, [P, P * PACK], BF16)
+            if j < PACK - 1:
+                w2_in[j] = sbuf("w2_in%d" % j, [P, P * PACK], BF16)
+            else:
+                w2_in[j] = placed("w2_last", [P, P * PACK], BF16, 0)
             nc.scalar.copy(
                 w2_in[j][:].rearrange("m (p t) -> m p t", t=PACK), w2_banks[j][:].rearrange("m (t p) -> m p t", t=PACK)
             )
@@ -138,6 +144,8 @@ def tile_attend_gnce_x_ts_kernel(tc, xT, wT, y, wt, ts, offs, out):
         group_w2(1)
         make_factor(0, 1)
         make_factor(0, 2)
+        for t in range(PACK):
+            make_factor(1, t)
         gather_w(2)
         turn_w(2)
         make_factor(0, 3)
@@ -148,48 +156,45 @@ def tile_attend_gnce_x_ts_kernel(tc, xT, wT, y, wt, ts, offs, out):
         x_view = xT[0].rearrange("(p j) r -> p j r", j=PACK)
         x_tiles = {}
         y_tiles = {}
-        x_pairs = {}
-        y_pairs = {}
+        half_plane = PLANE_BYTES // 2
+        quarter_plane = PLANE_BYTES // 4
 
-        def load_x(k):
-            if k % 2 == 0:
-                x_pairs[k // 2] = stage.tile([P, 2, PACK, CHUNK], F32, name="staged")
-            x_tiles[k] = x_pairs[k // 2][:, k % 2]
-            nc.sync.dma_start(x_tiles[k], x_view[:, :, k * CHUNK : (k + 1) * CHUNK])
+        def load_x(k, offset):
+            x_tiles[k] = placed("x_raw%d" % k, [P, PACK, CHUNK], F32, offset)
+            nc.sync.dma_start(x_tiles[k][:], x_view[:, :, k * CHUNK : (k + 1) * CHUNK])
 
-        def load_y(first, count):
-            if first % PACK == 0:
-                y_pairs[first // PACK] = stage.tile([P, PACK, N], F32, name="staged")
-            part = y_pairs[first // PACK][:, first % PACK : first % PACK + count, :]
+        def load_y(first, count, offset):
+            part = placed("y_raw%d" % first, [P, count, N], F32, offset)
             rows = y[0][first * BLOCK : (first + count) * BLOCK, :]
-            nc.sync.dma_start(part, rows.rearrange("(c p) i -> p c i", p=P))
+            nc.sync.dma_start(part[:], rows.rearrange("(c p) i -> p c i", p=P))
             for c in range(count):
                 y_tiles[first + c] = part[:, c, :]
 
-        load_x(0)
-        load_x(1)
-        load_x(2)
-        load_y(0, 1)
-        load_x(3)
-        load_y(1, 1)
-        load_y(2, 2)
-        load_y(4, 2)
-        load_y(6, 2)
+        load_x(0, 0)
+        load_x(1, half_plane)
+        load_x(2, PLANE_BYTES)
+        load_y(0, 1, PLANE_BYTES + 2 * quarter_plane)
+        load_y(1, 1, PLANE_BYTES + 3 * quarter_plane)
+        load_y(2, 1, 2 * PLANE_BYTES)
+        load_x(3, 2 * PLANE_BYTES + quarter_plane)
+        load_y(3, 1, 2 * PLANE_BYTES + 3 * quarter_plane)
+        load_y(4, 2, 3 * PLANE_BYTES + half_plane)
 
-        units = [(0, BLOCK), (BLOCK, BLOCK), (CHUNK, CHUNK), (2 * CHUNK, CHUNK), (3 * CHUNK, CHUNK)]
+        units = [(0, BLOCK), (BLOCK, BLOCK), (CHUNK, CHUNK), (2 * CHUNK, CHUNK), (6 * BLOCK, BLOCK), (7 * BLOCK, BLOCK)]
         x_in = {}
         x_codes = {}
         x_scales = {}
 
+        def sig_place(b):
+            return PACK * PLANE_BYTES + (n_blocks + b) * 4 * N
+
         def group_x(u, engine_copy):
             first, rows = units[u]
             k, skip = divmod(first, CHUNK)
-            if u == 0:
-                early = sbuf("shared", [P, 2 * CHUNK * PACK], BF16)
-                for v in range(3):
-                    x_in[v] = early[:, units[v][0] * PACK : (units[v][0] + units[v][1]) * PACK]
-            if u >= 3:
-                x_in[u] = sbuf("shared", [P, rows * PACK], BF16)[:]
+            if u >= 4:
+                x_in[u] = placed("x_in%d" % u, [P, rows * PACK], BF16, sig_place(u - X_HOLD))[:]
+            else:
+                x_in[u] = sbuf("x_in%d" % u, [P, rows * PACK], BF16)[:]
             engine_copy(
                 x_in[u].rearrange("p (c i j) -> p c j i", i=2, j=PACK),
                 x_tiles[k][:, :, skip : skip + rows].rearrange("p j (c i) -> p c j i", i=2),
@@ -201,14 +206,15 @@ def tile_attend_gnce_x_ts_kernel(tc, xT, wT, y, wt, ts, offs, out):
             x_scales[u] = sbuf("x_scales%d" % u, [P, rows], U8)
             nc.vector.quantize_mx(x_codes[u][:].bitcast(E4M3), x_scales[u][:], x_in[u])
 
-        w1_codes = {}
-        w1_scales = {}
+        w1_all = sbuf("w1_codes", [P, N], U32)
+        w1_all_scales = sbuf("w1_scales", [P, N], U8)
+        w1_codes = [w1_all[:, t * P : (t + 1) * P] for t in range(PACK)]
+        w1_scales = [w1_all_scales[:, t * P : (t + 1) * P] for t in range(PACK)]
 
         def quantise_w1(t):
-            w1_codes[t] = sbuf("w1_codes%d" % t, [P, P], U32)
-            w1_scales[t] = sbuf("w1_scales%d" % t, [P, P], U8)
+            cols = slice(t * P, (t + 2) * P)
             nc.vector.quantize_mx(
-                w1_codes[t][:].bitcast(E4M3), w1_scales[t][:], w1_in[:, t * P * PACK : (t + 1) * P * PACK]
+                w1_all[:, cols].bitcast(E4M3), w1_all_scales[:, cols], w1_in[:, t * P * PACK : (t + 2) * P * PACK]
             )
 
         sig = {}
@@ -217,36 +223,39 @@ def tile_attend_gnce_x_ts_kernel(tc, xT, wT, y, wt, ts, offs, out):
         h_codes = {}
         h_scales = {}
 
-        def scores(u, places, k):
-            first, rows = units[u]
-            if places[0] == 0:
-                tile = sbuf("sig%d" % u, [P, PACK, rows], F32)
-                for c in range(rows // BLOCK):
-                    sig[first // BLOCK + c] = tile[:, :, c * BLOCK : (c + 1) * BLOCK]
-                sig["unit", u] = tile
-            acc = bank(k)
-            for n, t in enumerate(places):
+        def scores(b):
+            u = max(v for v in range(len(units)) if units[v][0] <= b * BLOCK)
+            cols = slice(b * BLOCK - units[u][0], (b + 1) * BLOCK - units[u][0])
+            sig[b] = placed("sig%d" % b, [P, PACK, BLOCK], F32, sig_place(b))
+            acc = bank(b % 2)
+            for t in range(PACK):
                 nc.tensor.matmul_mx(
-                    acc[:, n * rows : (n + 1) * rows],
+                    acc[:, t * BLOCK : (t + 1) * BLOCK],
                     lhsT=w1_codes[t][:].bitcast(E4M3),
                     lhsT_scale=w1_scales[t][:],
-                    rhs=x_codes[u][:].bitcast(E4M3),
-                    rhs_scale=x_scales[u][:],
+                    rhs=x_codes[u][:, cols].bitcast(E4M3),
+                    rhs_scale=x_scales[u][:, cols],
                     start=True,
                     stop=True,
                 )
-            for n, t in enumerate(places):
+            for t in range(PACK):
                 nc.scalar.activation(
-                    sig["unit", u][:, t, :], acc[:, n * rows : (n + 1) * rows], ACT.Sigmoid, scale=ts_slot[:, t : t + 1]
+                    sig[b][:, t, :], acc[:, t * BLOCK : (t + 1) * BLOCK], ACT.Sigmoid, scale=ts_slot[:, t : t + 1]
                 )
 
+        def diff_place(b):
+            return PACK * PLANE_BYTES + b * 4 * N
+
         def quantise_h(b):
-            h_codes[b] = sbuf("h_codes%d" % b, [P, BLOCK], U32)
+            if b + 2 < n_blocks:
+                h_codes[b] = placed("h_codes%d" % b, [P, BLOCK], U32, diff_place(b + 1))
+            else:
+                h_codes[b] = sbuf("h_codes%d" % b, [P, BLOCK], U32)
             h_scales[b] = sbuf("h_scales%d" % b, [P, BLOCK], U8)
             nc.vector.quantize_mx(h_codes[b][:].bitcast(E5M2), h_scales[b][:], h_in[b][:])
 
         def gradient(b, engine_copy):
-            acc = bank(6 + b % 2)
+            acc = bank(OUT_BANKS[b])
             nc.tensor.matmul_mx(
                 acc[:],
                 lhsT=h_codes[b][:].bitcast(E5M2),
@@ -269,12 +278,9 @@ def tile_attend_gnce_x_ts_kernel(tc, xT, wT, y, wt, ts, offs, out):
 
         group_x(0, nc.scalar.copy)
         group_x(1, nc.scalar.copy)
-        group_x(2, nc.scalar.copy)
         quantise_w1(0)
-        quantise_w1(1)
         quantise_x(0)
         quantise_w1(2)
-        quantise_w1(3)
         quantise_x(1)
 
         sig_banks = {}
@@ -286,7 +292,7 @@ def tile_attend_gnce_x_ts_kernel(tc, xT, wT, y, wt, ts, offs, out):
                 nc.tensor.transpose(sig_banks[b][:, t * P : (t + 1) * P], sig[b][:, t, :], ident[:])
 
         def subtract(b):
-            diff[b] = sbuf("diff%d" % b, [P, PACK, P], F32)
+            diff[b] = placed("diff%d" % b, [P, PACK, P], F32, diff_place(b))
             nc.vector.tensor_tensor(
                 diff[b][:].rearrange("r t (c i) -> r c t i", i=2),
                 sig_banks[b][:].rearrange("r (t c i) -> r c t i", t=PACK, i=2),
@@ -308,40 +314,31 @@ def tile_attend_gnce_x_ts_kernel(tc, xT, wT, y, wt, ts, offs, out):
                 ALU.mult,
             )
 
-        scores(0, [0, 1, 2, 3], 0)
-        scores(1, [0, 1, 2, 3], 1)
-        quantise_x(2)
+        scores(0)
+        scores(1)
         for j in range(PACK - 1):
             quantise_w2(j)
+        group_x(2, nc.vector.tensor_copy)
+        load_y(6, 2, half_plane)
+        group_w2(3)
+        quantise_w2(3)
+        quantise_x(2)
         group_x(3, nc.vector.tensor_copy)
         quantise_x(3)
-        turn_sig(0)
-        scores(2, [0, 1], 0)
-        turn_sig(1)
-        scores(2, [2, 3], 1)
-        group_w2(3)
-        for s in range(-2, n_blocks + 2):
-            if s >= 2:
-                gradient(s - 2, nc.vector.tensor_copy if s == n_blocks + 1 else nc.scalar.copy)
-            if s in (-1, 0):
-                scores(3, [2 * s + 2, 2 * s + 3], s + 1)
-            if s in (1, 2):
-                scores(4, [2 * s - 2, 2 * s - 1], s - 1)
-            if 0 <= s < PACK:
-                make_factor(1, s)
+        for s in range(-4, n_blocks + 1):
             if 0 <= s + 1 < n_blocks:
                 turn_diff(s + 1)
-            if 2 <= s + 3 < n_blocks:
-                turn_sig(s + 3)
-            if s + 2 < n_blocks:
+            if 0 <= s + 2 < n_blocks:
                 subtract(s + 2)
-            if s == -1:
-                quantise_w2(3)
-            if s == -1:
-                group_x(4, nc.vector.tensor_copy)
-            if 1 <= s <= n_blocks:
-                quantise_h(s - 1)
+            if 0 <= s + SIG_LEAD < n_blocks:
+                turn_sig(s + SIG_LEAD)
+            if s in (X4_STEP, X4_STEP + 1):
+                group_x(4 + s - X4_STEP, nc.scalar.copy)
+                quantise_x(4 + s - X4_STEP)
+            if 2 <= s + SCORE_LEAD < n_blocks:
+                scores(s + SCORE_LEAD)
             if 0 <= s < n_blocks:
                 weigh(s)
-            if s == 0:
-                quantise_x(4)
+            if s >= 1:
+                quantise_h(s - 1)
+                gradient(s - 1, nc.vector.tensor_copy if s == n_blocks else nc.scalar.copy)

@@ -14,6 +14,10 @@ SCORE_LEAD = 5
 X4_STEP = -1
 PLANE_BYTES = 4 * T
 X_HOLD = 2
+G_LAG = 1
+H_HOLD = 2
+F2_PLACE = PLANE_BYTES + PLANE_BYTES // 4
+F2_STEP = -2
 W2_PLACE = (PACK - 1) * PLANE_BYTES
 FLOPS = 2 * 2 * R * N * D
 BYTES = 4 * (D * R + D * T + R * N + R + T + R * D) + 2 * P * (N // 16)
@@ -21,7 +25,6 @@ BYTES = 4 * (D * R + D * T + R * N + R + T + R * D) + 2 * P * (N // 16)
 F32 = mybir.dt.float32
 BF16 = mybir.dt.bfloat16
 U32 = mybir.dt.uint32
-I32 = mybir.dt.int32
 U16 = mybir.dt.uint16
 U8 = mybir.dt.uint8
 E4M3 = mybir.dt.float8_e4m3fn_x4
@@ -47,6 +50,8 @@ def tile_attend_gnce_x_ts_kernel(tc, xT, wT, y, wt, ts, offs, out):
 
         offsets = keep.tile([P, N // 16], U16, name="offsets")
         nc.sync.dma_start(offsets[:], offs)
+        ts_rows = sbuf("ts_rows", [P, 16], F32)
+        nc.scalar.dma_start(ts_rows[:], ts[0].rearrange("(p c) -> p c", c=16))
         wt_rows = sbuf("wt_rows", [P, 8], F32)
         nc.scalar.dma_start(
             wt_rows[:].rearrange("p (h c) -> p h c", h=2), wt[0].rearrange("(h p c) o -> p h (c o)", h=2, c=4)
@@ -55,26 +60,36 @@ def tile_attend_gnce_x_ts_kernel(tc, xT, wT, y, wt, ts, offs, out):
         def placed(name, shape, dtype, offset):
             return stage.tile(shape, dtype, name=name, offset=offset, align_bytes=64)
 
-        ts_table = sbuf("ts_table", [P, T], F32)
-        nc.vector.memset(ts_table[:].bitcast(I32), 0)
-        warm = placed("warm", [P, (PACK - 1) * T], F32, PLANE_BYTES)
-        nc.scalar.activation(warm[P // 2 :, 0:1], ts_table[P // 2 :, 0:1], ACT.Sigmoid)
-
         w_view = wT.rearrange("(p j) t -> p j t", j=PACK)
         w_planes = []
         for j in range(PACK):
             plane = placed("plane%d" % j, [P, T], F32, j * PLANE_BYTES)
             nc.sync.dma_start(plane[:], w_view[:, j, :])
             w_planes.append(plane)
-            if j == 0:
-                nc.sync.dma_start(ts_table[0:1, :], ts[0:1, :])
 
         ident = sbuf("ident", [P, P], F32)
         make_identity(nc, ident[:])
         ident_bf = sbuf("ident_bf", [P, P], BF16)
         make_identity(nc, ident_bf[:])
 
-        factor = [sbuf("factor%d" % n, [P, PACK, R // 2], F32) for n in range(2)]
+        warm = sbuf("warm", [P, 1], F32)
+        nc.scalar.activation(warm[:], ts_rows[:, 0:1], ACT.Sigmoid)
+
+        ts_table = sbuf("ts_table", [P, T], F32)
+        for g in range(4):
+            spread = bank(g)
+            for c in range(4):
+                col = 4 * g + c
+                nc.tensor.transpose(
+                    spread[:, c * P : (c + 1) * P], ts_rows[:, col : col + 1].to_broadcast([P, P]), ident[:]
+                )
+            copy_out = nc.scalar.copy if g % 2 == 0 else nc.vector.tensor_copy
+            copy_out(
+                ts_table[:].rearrange("m (p g c) -> m g p c", g=4, c=4)[:, g],
+                spread[:].rearrange("m (c p) -> m p c", c=4),
+            )
+
+        factor = {}
         wt_wide = [sbuf("wt_wide%d" % n, [P, R // 2], F32) for n in range(2)]
         for h in range(2):
             wt_bank = bank(4 + h)
@@ -96,11 +111,23 @@ def tile_attend_gnce_x_ts_kernel(tc, xT, wT, y, wt, ts, offs, out):
         ts_slot = sbuf("ts_slot", [P, PACK], F32)
         nc.scalar.copy(ts_slot[:], ts_bank[:, 0::P])
 
-        def make_factor(half, t):
-            if half == 0:
+        def make_factor(k, t):
+            if k == 0:
+                if t == 0:
+                    factor[0] = sbuf("factor0", [P, PACK, 2 * CHUNK], F32)
                 nc.scalar.activation(factor[0][:, t, :], wt_wide[0][:], ACT.Copy, scale=ts_slot[:, t : t + 1])
-            else:
-                nc.vector.tensor_scalar(factor[1][:, t, :], wt_wide[1][:], ts_slot[:, t : t + 1], None, ALU.mult)
+                return
+            if t == 0 and k == 1:
+                factor[1] = sbuf("factor1", [P, PACK, CHUNK], F32)
+            if t == 0 and k == 2:
+                factor[2] = placed("factor2", [P, PACK, CHUNK], F32, F2_PLACE)
+            nc.vector.tensor_scalar(
+                factor[k][:, t, :], wt_wide[1][:, (k - 1) * CHUNK : k * CHUNK], ts_slot[:, t : t + 1], None, ALU.mult
+            )
+
+        def factor_of(b):
+            k, first = (0, 0) if b < 4 else (b // 2 - 1, b // 2 * 2)
+            return factor[k][:, :, (b - first) * BLOCK : (b - first + 1) * BLOCK]
 
         w1_in = sbuf("ts_table", [P, N * PACK], BF16)
         w2_codes = placed("w2_codes", [P, D], U32, W2_PLACE)
@@ -122,36 +149,30 @@ def tile_attend_gnce_x_ts_kernel(tc, xT, wT, y, wt, ts, offs, out):
             w2_banks[j] = turned
 
         def group_w2(j):
-            if j < PACK - 1:
-                w2_in[j] = sbuf("w2_in%d" % j, [P, P * PACK], BF16)
-            else:
-                w2_in[j] = placed("w2_last", [P, P * PACK], BF16, 0)
+            if j == 0:
+                w2_in[0] = sbuf("w2_in0", [P, 2, P * PACK], BF16)
+            if j == 2:
+                w2_in[1] = placed("w2_in1", [P, 2, P * PACK], BF16, 0)
             nc.scalar.copy(
-                w2_in[j][:].rearrange("m (p t) -> m p t", t=PACK), w2_banks[j][:].rearrange("m (t p) -> m p t", t=PACK)
+                w2_in[j // 2][:, j % 2, :].rearrange("m (p t) -> m p t", t=PACK), w2_banks[j][:].rearrange("m (t p) -> m p t", t=PACK)
             )
 
-        def quantise_w2(j):
+        def quantise_w2(n):
+            cols = slice(2 * n * P, 2 * (n + 1) * P)
             nc.vector.quantize_mx(
-                w2_codes[:, j * P : (j + 1) * P].bitcast(E4M3), w2_scales[:, j * P : (j + 1) * P], w2_in[j][:]
+                w2_codes[:, cols].bitcast(E4M3), w2_scales[:, cols], w2_in[n][:].rearrange("m j c -> m (j c)")
             )
 
-        gather_w(0)
-        turn_w(0)
-        group_w2(0)
-        make_factor(0, 0)
-        gather_w(1)
-        turn_w(1)
-        group_w2(1)
-        make_factor(0, 1)
-        make_factor(0, 2)
         for t in range(PACK):
-            make_factor(1, t)
-        gather_w(2)
-        turn_w(2)
-        make_factor(0, 3)
-        group_w2(2)
-        gather_w(3)
-        turn_w(3)
+            make_factor(0, t)
+        for j in range(PACK):
+            if j == PACK - 1:
+                for t in range(PACK):
+                    make_factor(1, t)
+            gather_w(j)
+            turn_w(j)
+            if j < 2:
+                group_w2(j)
 
         x_view = xT[0].rearrange("(p j) r -> p j r", j=PACK)
         x_tiles = {}
@@ -247,7 +268,7 @@ def tile_attend_gnce_x_ts_kernel(tc, xT, wT, y, wt, ts, offs, out):
             return PACK * PLANE_BYTES + b * 4 * N
 
         def quantise_h(b):
-            if b + 2 < n_blocks:
+            if b + H_HOLD < n_blocks:
                 h_codes[b] = placed("h_codes%d" % b, [P, BLOCK], U32, diff_place(b + 1))
             else:
                 h_codes[b] = sbuf("h_codes%d" % b, [P, BLOCK], U32)
@@ -310,26 +331,29 @@ def tile_attend_gnce_x_ts_kernel(tc, xT, wT, y, wt, ts, offs, out):
             nc.vector.tensor_tensor(
                 h_in[b][:].rearrange("m (c i t) -> m c t i", i=2, t=PACK),
                 diff_banks[b][:].rearrange("m (t c i) -> m c t i", t=PACK, i=2),
-                factor[b // 4][:, :, b % 4 * BLOCK : (b % 4 + 1) * BLOCK].rearrange("m t (c i) -> m c t i", i=2),
+                factor_of(b).rearrange("m t (c i) -> m c t i", i=2),
                 ALU.mult,
             )
 
         scores(0)
         scores(1)
-        for j in range(PACK - 1):
-            quantise_w2(j)
+        quantise_w2(0)
         group_x(2, nc.vector.tensor_copy)
         load_y(6, 2, half_plane)
+        group_w2(2)
         group_w2(3)
-        quantise_w2(3)
         quantise_x(2)
         group_x(3, nc.vector.tensor_copy)
+        quantise_w2(1)
         quantise_x(3)
-        for s in range(-4, n_blocks + 1):
+        for s in range(-4, n_blocks + G_LAG):
             if 0 <= s + 1 < n_blocks:
                 turn_diff(s + 1)
             if 0 <= s + 2 < n_blocks:
                 subtract(s + 2)
+            if s == F2_STEP:
+                for t in range(PACK):
+                    make_factor(2, t)
             if 0 <= s + SIG_LEAD < n_blocks:
                 turn_sig(s + SIG_LEAD)
             if s in (X4_STEP, X4_STEP + 1):
@@ -339,6 +363,7 @@ def tile_attend_gnce_x_ts_kernel(tc, xT, wT, y, wt, ts, offs, out):
                 scores(s + SCORE_LEAD)
             if 0 <= s < n_blocks:
                 weigh(s)
-            if s >= 1:
+            if 1 <= s <= n_blocks:
                 quantise_h(s - 1)
-                gradient(s - 1, nc.vector.tensor_copy if s == n_blocks else nc.scalar.copy)
+            if 0 <= s - G_LAG < n_blocks:
+                gradient(s - G_LAG, nc.vector.tensor_copy if s - G_LAG == n_blocks - 1 else nc.scalar.copy)

@@ -15,9 +15,10 @@ X4_STEP = -1
 PLANE_BYTES = 4 * T
 X_HOLD = 2
 G_LAG = 1
-H_HOLD = 2
-F2_PLACE = PLANE_BYTES + PLANE_BYTES // 4
-F2_STEP = -2
+H_HOLD = 3
+F2_HOLD = 5
+F2_STEP = 3
+WT_PLACE = PACK * PLANE_BYTES + 2 * (R // BLOCK) * 4 * N
 W2_PLACE = (PACK - 1) * PLANE_BYTES
 FLOPS = 2 * 2 * R * N * D
 BYTES = 4 * (D * R + D * T + R * N + R + T + R * D) + 2 * P * (N // 16)
@@ -83,14 +84,13 @@ def tile_attend_gnce_x_ts_kernel(tc, xT, wT, y, wt, ts, offs, out):
                 nc.tensor.transpose(
                     spread[:, c * P : (c + 1) * P], ts_rows[:, col : col + 1].to_broadcast([P, P]), ident[:]
                 )
-            copy_out = nc.scalar.copy if g % 2 == 0 else nc.vector.tensor_copy
-            copy_out(
+            nc.scalar.copy(
                 ts_table[:].rearrange("m (p g c) -> m g p c", g=4, c=4)[:, g],
                 spread[:].rearrange("m (c p) -> m p c", c=4),
             )
 
         factor = {}
-        wt_wide = [sbuf("wt_wide%d" % n, [P, R // 2], F32) for n in range(2)]
+        wt_wide = [placed("wt_early", [P, R // 2], F32, WT_PLACE), sbuf("wt_late", [P, R // 2], F32)]
         for h in range(2):
             wt_bank = bank(4 + h)
             for c in range(4):
@@ -103,6 +103,8 @@ def tile_attend_gnce_x_ts_kernel(tc, xT, wT, y, wt, ts, offs, out):
                 wt_bank[:].rearrange("m (c p) -> m p c", c=4),
             )
 
+        first_plane = sbuf("first_plane", [P, N], F32)
+        nc.vector.tensor_copy(first_plane[:], w_planes[0][:].indirect(offsets[:]))
         ts_listed = sbuf("ts_listed", [P, N], F32)
         nc.vector.tensor_copy(ts_listed[:], ts_table[:].indirect(offsets[:]))
         ts_bank = bank(0)
@@ -118,9 +120,12 @@ def tile_attend_gnce_x_ts_kernel(tc, xT, wT, y, wt, ts, offs, out):
                 nc.scalar.activation(factor[0][:, t, :], wt_wide[0][:], ACT.Copy, scale=ts_slot[:, t : t + 1])
                 return
             if t == 0 and k == 1:
-                factor[1] = sbuf("factor1", [P, PACK, CHUNK], F32)
+                factor[1] = placed("factor1", [P, PACK, CHUNK], F32, PLANE_BYTES + PLANE_BYTES // 2)
             if t == 0 and k == 2:
-                factor[2] = placed("factor2", [P, PACK, CHUNK], F32, F2_PLACE)
+                factor[2] = placed("factor2", [P, PACK, CHUNK], F32, PACK * PLANE_BYTES + (n_blocks + F2_HOLD) * 4 * N)
+            if k == 2:
+                nc.scalar.activation(factor[2][:, t, :], wt_wide[1][:, CHUNK:], ACT.Copy, scale=ts_slot[:, t : t + 1])
+                return
             nc.vector.tensor_scalar(
                 factor[k][:, t, :], wt_wide[1][:, (k - 1) * CHUNK : k * CHUNK], ts_slot[:, t : t + 1], None, ALU.mult
             )
@@ -130,7 +135,6 @@ def tile_attend_gnce_x_ts_kernel(tc, xT, wT, y, wt, ts, offs, out):
             return factor[k][:, :, (b - first) * BLOCK : (b - first + 1) * BLOCK]
 
         w1_in = sbuf("ts_table", [P, N * PACK], BF16)
-        w2_codes = placed("w2_codes", [P, D], U32, W2_PLACE)
         w2_scales = sbuf("w2_scales", [P, D], U8)
         w2_in = {}
         w2_banks = {}
@@ -138,7 +142,7 @@ def tile_attend_gnce_x_ts_kernel(tc, xT, wT, y, wt, ts, offs, out):
         def gather_w(j):
             nc.vector.tensor_copy(
                 w1_in[:].rearrange("p (t m j) -> p j m t", t=PACK, j=PACK)[:, j],
-                w_planes[j][:].indirect(offsets[:]),
+                first_plane[:].rearrange("p (m t) -> p m t", t=PACK) if j == 0 else w_planes[j][:].indirect(offsets[:]),
             )
 
         def turn_w(j):
@@ -166,9 +170,6 @@ def tile_attend_gnce_x_ts_kernel(tc, xT, wT, y, wt, ts, offs, out):
         for t in range(PACK):
             make_factor(0, t)
         for j in range(PACK):
-            if j == PACK - 1:
-                for t in range(PACK):
-                    make_factor(1, t)
             gather_w(j)
             turn_w(j)
             if j < 2:
@@ -212,7 +213,9 @@ def tile_attend_gnce_x_ts_kernel(tc, xT, wT, y, wt, ts, offs, out):
         def group_x(u, engine_copy):
             first, rows = units[u]
             k, skip = divmod(first, CHUNK)
-            if u >= 4:
+            if u < 4:
+                x_in[u] = placed("x_in%d" % u, [P, rows * PACK], BF16, WT_PLACE + (u == 1) * 2 * BLOCK * PACK)[:]
+            elif u >= 4:
                 x_in[u] = placed("x_in%d" % u, [P, rows * PACK], BF16, sig_place(u - X_HOLD))[:]
             else:
                 x_in[u] = sbuf("x_in%d" % u, [P, rows * PACK], BF16)[:]
@@ -223,7 +226,10 @@ def tile_attend_gnce_x_ts_kernel(tc, xT, wT, y, wt, ts, offs, out):
 
         def quantise_x(u):
             rows = units[u][1]
-            x_codes[u] = sbuf("x_codes%d" % u, [P, rows], U32)
+            if u < 2:
+                x_codes[u] = placed("x_codes%d" % u, [P, rows], U32, W2_PLACE + 4 * D + u * 4 * BLOCK)
+            else:
+                x_codes[u] = sbuf("x_codes%d" % u, [P, rows], U32)
             x_scales[u] = sbuf("x_scales%d" % u, [P, rows], U8)
             nc.vector.quantize_mx(x_codes[u][:].bitcast(E4M3), x_scales[u][:], x_in[u])
 
@@ -335,15 +341,16 @@ def tile_attend_gnce_x_ts_kernel(tc, xT, wT, y, wt, ts, offs, out):
                 ALU.mult,
             )
 
-        scores(0)
-        scores(1)
-        quantise_w2(0)
-        group_x(2, nc.vector.tensor_copy)
-        load_y(6, 2, half_plane)
         group_w2(2)
         group_w2(3)
+        scores(0)
+        scores(1)
+        w2_codes = placed("w2_codes", [P, D], U32, PLANE_BYTES // 4)
+        quantise_w2(0)
+        group_x(2, nc.vector.tensor_copy)
         quantise_x(2)
         group_x(3, nc.vector.tensor_copy)
+        load_y(6, 2, PLANE_BYTES)
         quantise_w2(1)
         quantise_x(3)
         for s in range(-4, n_blocks + G_LAG):
@@ -351,11 +358,14 @@ def tile_attend_gnce_x_ts_kernel(tc, xT, wT, y, wt, ts, offs, out):
                 turn_diff(s + 1)
             if 0 <= s + 2 < n_blocks:
                 subtract(s + 2)
+            if 0 <= s + SIG_LEAD < n_blocks:
+                turn_sig(s + SIG_LEAD)
+            if s == -1:
+                for t in range(PACK):
+                    make_factor(1, t)
             if s == F2_STEP:
                 for t in range(PACK):
                     make_factor(2, t)
-            if 0 <= s + SIG_LEAD < n_blocks:
-                turn_sig(s + SIG_LEAD)
             if s in (X4_STEP, X4_STEP + 1):
                 group_x(4 + s - X4_STEP, nc.scalar.copy)
                 quantise_x(4 + s - X4_STEP)

@@ -52,11 +52,8 @@ def tile_attend_gnce_x_ts_kernel(tc, xT, wT, y, wt, ts, offs, out):
         offsets = keep.tile([P, N // 16], U16, name="offsets")
         nc.sync.dma_start(offsets[:], offs)
         ts_rows = sbuf("ts_rows", [P, 16], F32)
-        nc.scalar.dma_start(ts_rows[:], ts[0].rearrange("(p c) -> p c", c=16))
+        nc.sync.dma_start(ts_rows[:], ts[0].rearrange("(p c) -> p c", c=16))
         wt_rows = sbuf("wt_rows", [P, 8], F32)
-        nc.scalar.dma_start(
-            wt_rows[:].rearrange("p (h c) -> p h c", h=2), wt[0].rearrange("(h p c) o -> p h (c o)", h=2, c=4)
-        )
 
         def placed(name, shape, dtype, offset):
             return stage.tile(shape, dtype, name=name, offset=offset, align_bytes=64)
@@ -67,6 +64,10 @@ def tile_attend_gnce_x_ts_kernel(tc, xT, wT, y, wt, ts, offs, out):
             plane = placed("plane%d" % j, [P, T], F32, j * PLANE_BYTES)
             nc.sync.dma_start(plane[:], w_view[:, j, :])
             w_planes.append(plane)
+            if j == 0:
+                nc.sync.dma_start(
+                    wt_rows[:].rearrange("p (h c) -> p h c", h=2), wt[0].rearrange("(h p c) o -> p h (c o)", h=2, c=4)
+                )
 
         ident = sbuf("ident", [P, P], F32)
         make_identity(nc, ident[:])

@@ -19,7 +19,8 @@ H_HOLD = 3
 F2_HOLD = 5
 F2_STEP = 3
 WT_PLACE = PACK * PLANE_BYTES + 2 * (R // BLOCK) * 4 * N
-W2_PLACE = (PACK - 1) * PLANE_BYTES
+LAST_PLACE = WT_PLACE + 2 * PLANE_BYTES
+W2_PLACE = LAST_PLACE
 FLOPS = 2 * 2 * R * N * D
 BYTES = 4 * (D * R + D * T + R * N + R + T + R * D) + 2 * P * (N // 16)
 
@@ -61,6 +62,8 @@ def tile_attend_gnce_x_ts_kernel(tc, xT, wT, y, wt, ts, offs, out):
         w_view = wT.rearrange("(p j) t -> p j t", j=PACK)
         w_planes = []
         for j in range(PACK):
+            if j == PACK - 1:
+                break
             plane = placed("plane%d" % j, [P, T], F32, j * PLANE_BYTES)
             nc.sync.dma_start(plane[:], w_view[:, j, :])
             w_planes.append(plane)
@@ -77,7 +80,7 @@ def tile_attend_gnce_x_ts_kernel(tc, xT, wT, y, wt, ts, offs, out):
         warm = sbuf("warm", [P, 1], F32)
         nc.scalar.activation(warm[:], ts_rows[:, 0:1], ACT.Sigmoid)
 
-        ts_table = sbuf("ts_table", [P, T], F32)
+        ts_table = placed("ts_table", [P, T], F32, LAST_PLACE - 64)
         for g in range(4):
             spread = bank(g)
             for c in range(4):
@@ -85,7 +88,7 @@ def tile_attend_gnce_x_ts_kernel(tc, xT, wT, y, wt, ts, offs, out):
                 nc.tensor.transpose(
                     spread[:, c * P : (c + 1) * P], ts_rows[:, col : col + 1].to_broadcast([P, P]), ident[:]
                 )
-            nc.scalar.copy(
+            (nc.vector.tensor_copy if g % 2 else nc.scalar.copy)(
                 ts_table[:].rearrange("m (p g c) -> m g p c", g=4, c=4)[:, g],
                 spread[:].rearrange("m (c p) -> m p c", c=4),
             )
@@ -104,10 +107,11 @@ def tile_attend_gnce_x_ts_kernel(tc, xT, wT, y, wt, ts, offs, out):
                 wt_bank[:].rearrange("m (c p) -> m p c", c=4),
             )
 
-        first_plane = sbuf("first_plane", [P, N], F32)
-        nc.vector.tensor_copy(first_plane[:], w_planes[0][:].indirect(offsets[:]))
         ts_listed = sbuf("ts_listed", [P, N], F32)
         nc.vector.tensor_copy(ts_listed[:], ts_table[:].indirect(offsets[:]))
+        last_plane = placed("plane3", [P, T], F32, LAST_PLACE)
+        nc.sync.dma_start(last_plane[:], w_view[:, PACK - 1, :])
+        w_planes.append(last_plane)
         ts_bank = bank(0)
         for t in range(PACK):
             nc.tensor.transpose(ts_bank[:, t * P : (t + 1) * P], ts_listed[:, t::PACK], ident[:])
@@ -121,7 +125,7 @@ def tile_attend_gnce_x_ts_kernel(tc, xT, wT, y, wt, ts, offs, out):
                 nc.scalar.activation(factor[0][:, t, :], wt_wide[0][:], ACT.Copy, scale=ts_slot[:, t : t + 1])
                 return
             if t == 0 and k == 1:
-                factor[1] = placed("factor1", [P, PACK, CHUNK], F32, PLANE_BYTES + PLANE_BYTES // 2)
+                factor[1] = sbuf("factor1", [P, PACK, CHUNK], F32)
             if t == 0 and k == 2:
                 factor[2] = placed("factor2", [P, PACK, CHUNK], F32, PACK * PLANE_BYTES + (n_blocks + F2_HOLD) * 4 * N)
             if k == 2:
@@ -135,7 +139,7 @@ def tile_attend_gnce_x_ts_kernel(tc, xT, wT, y, wt, ts, offs, out):
             k, first = (0, 0) if b < 4 else (b // 2 - 1, b // 2 * 2)
             return factor[k][:, :, (b - first) * BLOCK : (b - first + 1) * BLOCK]
 
-        w1_in = sbuf("ts_table", [P, N * PACK], BF16)
+        w1_in = placed("w1_in", [P, N * PACK], BF16, LAST_PLACE - 2 * N * PACK)
         w2_scales = sbuf("w2_scales", [P, D], U8)
         w2_in = {}
         w2_banks = {}
@@ -143,7 +147,7 @@ def tile_attend_gnce_x_ts_kernel(tc, xT, wT, y, wt, ts, offs, out):
         def gather_w(j):
             nc.vector.tensor_copy(
                 w1_in[:].rearrange("p (t m j) -> p j m t", t=PACK, j=PACK)[:, j],
-                first_plane[:].rearrange("p (m t) -> p m t", t=PACK) if j == 0 else w_planes[j][:].indirect(offsets[:]),
+                w_planes[j][:].indirect(offsets[:]),
             )
 
         def turn_w(j):
@@ -171,6 +175,9 @@ def tile_attend_gnce_x_ts_kernel(tc, xT, wT, y, wt, ts, offs, out):
         for t in range(PACK):
             make_factor(0, t)
         for j in range(PACK):
+            if j == PACK - 1:
+                for t in range(PACK):
+                    make_factor(1, t)
             gather_w(j)
             turn_w(j)
             if j < 2:
@@ -201,7 +208,7 @@ def tile_attend_gnce_x_ts_kernel(tc, xT, wT, y, wt, ts, offs, out):
         load_y(2, 1, 2 * PLANE_BYTES)
         load_x(3, 2 * PLANE_BYTES + quarter_plane)
         load_y(3, 1, 2 * PLANE_BYTES + 3 * quarter_plane)
-        load_y(4, 2, 3 * PLANE_BYTES + half_plane)
+        load_y(4, 2, LAST_PLACE + half_plane)
 
         units = [(0, BLOCK), (BLOCK, BLOCK), (CHUNK, CHUNK), (2 * CHUNK, CHUNK), (6 * BLOCK, BLOCK), (7 * BLOCK, BLOCK)]
         x_in = {}
@@ -361,9 +368,6 @@ def tile_attend_gnce_x_ts_kernel(tc, xT, wT, y, wt, ts, offs, out):
                 subtract(s + 2)
             if 0 <= s + SIG_LEAD < n_blocks:
                 turn_sig(s + SIG_LEAD)
-            if s == -1:
-                for t in range(PACK):
-                    make_factor(1, t)
             if s == F2_STEP:
                 for t in range(PACK):
                     make_factor(2, t)

@@ -6,21 +6,14 @@ from concourse.masks import make_identity
 N, T, D, R = 512, 2048, 512, 1024
 P = 128
 PACK = 4
+RUN = 8
 BLOCK = 128
 CHUNK = 256
-OUT_BANKS = (6, 7, 6, 7, 6, 7, 0, 1)
-SIG_LEAD = 3
-SCORE_LEAD = 5
-X4_STEP = -1
+HALF = 64
+LEAD = 2
 PLANE_BYTES = 4 * T
-X_HOLD = 2
-G_LAG = 1
-H_HOLD = 3
-F2_HOLD = 5
-F2_STEP = 3
-WT_PLACE = PACK * PLANE_BYTES + 2 * (R // BLOCK) * 4 * N
-LAST_PLACE = WT_PLACE + 2 * PLANE_BYTES
-W2_PLACE = LAST_PLACE
+TILE_BYTES = 4 * N
+W1_PLACE = PACK * PLANE_BYTES
 FLOPS = 2 * 2 * R * N * D
 BYTES = 4 * (D * R + D * T + R * N + R + T + R * D) + 2 * P * (N // 16)
 
@@ -47,30 +40,28 @@ def tile_attend_gnce_x_ts_kernel(tc, xT, wT, y, wt, ts, offs, out):
         def sbuf(name, shape, dtype):
             return keep.tile(shape, dtype, name=name, align_bytes=64)
 
+        def placed(name, shape, dtype, offset):
+            return stage.tile(shape, dtype, name=name, offset=offset, align_bytes=64)
+
         def bank(k, dtype=F32):
             return psum.tile([P, 512], dtype, name="bank%d" % k)
 
         offsets = keep.tile([P, N // 16], U16, name="offsets")
         nc.sync.dma_start(offsets[:], offs)
-        ts_rows = sbuf("ts_rows", [P, 16], F32)
-        nc.sync.dma_start(ts_rows[:], ts[0].rearrange("(p c) -> p c", c=16))
+        ts_table = sbuf("ts_table", [P, T], F32)
+        nc.scalar.dma_start(ts_table[P - 1 : P, :], ts[0:1, :])
         wt_rows = sbuf("wt_rows", [P, 8], F32)
-
-        def placed(name, shape, dtype, offset):
-            return stage.tile(shape, dtype, name=name, offset=offset, align_bytes=64)
+        nc.sync.dma_start(
+            wt_rows[:].rearrange("p (h c) -> p h c", h=2), wt[0].rearrange("(h p c) o -> p h (c o)", h=2, c=4)
+        )
+        nc.vector.memset(ts_table[0 : P - 1, :], 0.0)
 
         w_view = wT.rearrange("(p j) t -> p j t", j=PACK)
         w_planes = []
         for j in range(PACK):
-            if j == PACK - 1:
-                break
             plane = placed("plane%d" % j, [P, T], F32, j * PLANE_BYTES)
             nc.sync.dma_start(plane[:], w_view[:, j, :])
             w_planes.append(plane)
-            if j == 0:
-                nc.sync.dma_start(
-                    wt_rows[:].rearrange("p (h c) -> p h c", h=2), wt[0].rearrange("(h p c) o -> p h (c o)", h=2, c=4)
-                )
 
         ident = sbuf("ident", [P, P], F32)
         make_identity(nc, ident[:])
@@ -78,75 +69,56 @@ def tile_attend_gnce_x_ts_kernel(tc, xT, wT, y, wt, ts, offs, out):
         make_identity(nc, ident_bf[:])
 
         warm = sbuf("warm", [P, 1], F32)
-        nc.scalar.activation(warm[:], ts_rows[:, 0:1], ACT.Sigmoid)
+        nc.scalar.activation(warm[:], ident[:, 0:1], ACT.Sigmoid)
 
-        ts_table = placed("ts_table", [P, T], F32, LAST_PLACE - 64)
-        for g in range(4):
-            spread = bank(g)
-            for c in range(4):
-                col = 4 * g + c
-                nc.tensor.transpose(
-                    spread[:, c * P : (c + 1) * P], ts_rows[:, col : col + 1].to_broadcast([P, P]), ident[:]
-                )
-            (nc.vector.tensor_copy if g % 2 else nc.scalar.copy)(
-                ts_table[:].rearrange("m (p g c) -> m g p c", g=4, c=4)[:, g],
-                spread[:].rearrange("m (c p) -> m p c", c=4),
-            )
-
-        factor = {}
-        wt_wide = [placed("wt_early", [P, R // 2], F32, WT_PLACE), sbuf("wt_late", [P, R // 2], F32)]
+        factor = sbuf("factor", [P, PACK, R], F32)
+        wt_banks = []
         for h in range(2):
-            wt_bank = bank(4 + h)
+            wt_bank = bank(2 + h)
             for c in range(4):
                 col = 4 * h + c
                 nc.tensor.transpose(
                     wt_bank[:, c * P : (c + 1) * P], wt_rows[:, col : col + 1].to_broadcast([P, P]), ident[:]
                 )
-            nc.scalar.copy(
-                wt_wide[h][:].rearrange("m (p c) -> m p c", c=4),
-                wt_bank[:].rearrange("m (c p) -> m p c", c=4),
-            )
+            wt_banks.append(wt_bank)
 
         ts_listed = sbuf("ts_listed", [P, N], F32)
-        nc.vector.tensor_copy(ts_listed[:], ts_table[:].indirect(offsets[:]))
-        last_plane = placed("plane3", [P, T], F32, LAST_PLACE)
-        nc.sync.dma_start(last_plane[:], w_view[:, PACK - 1, :])
-        w_planes.append(last_plane)
+        nc.vector.tensor_copy(
+            ts_listed[:].rearrange("p (t q e) -> p q t e", t=PACK, e=RUN), ts_table[:].indirect(offsets[:])
+        )
         ts_bank = bank(0)
         for t in range(PACK):
-            nc.tensor.transpose(ts_bank[:, t * P : (t + 1) * P], ts_listed[:, t::PACK], ident[:])
+            nc.tensor.transpose(ts_bank[:, t * P : (t + 1) * P], ts_listed[:, t * P : (t + 1) * P], ident[:])
         ts_slot = sbuf("ts_slot", [P, PACK], F32)
-        nc.scalar.copy(ts_slot[:], ts_bank[:, 0::P])
+        nc.scalar.copy(ts_slot[:], ts_bank[:, P - 1 :: P])
 
-        def make_factor(k, t):
-            if k == 0:
-                if t == 0:
-                    factor[0] = sbuf("factor0", [P, PACK, 2 * CHUNK], F32)
-                nc.scalar.activation(factor[0][:, t, :], wt_wide[0][:], ACT.Copy, scale=ts_slot[:, t : t + 1])
+        def make_factor(h, t):
+            if h == 1 and t < 2:
+                nc.vector.tensor_scalar(
+                    factor[:, t, h * 512 : (h + 1) * 512].rearrange("m (p c) -> m p c", c=4),
+                    wt_banks[h][:].rearrange("m (c p) -> m p c", c=4),
+                    ts_slot[:, t : t + 1],
+                    None,
+                    ALU.mult,
+                )
                 return
-            if t == 0 and k == 1:
-                factor[1] = sbuf("factor1", [P, PACK, CHUNK], F32)
-            if t == 0 and k == 2:
-                factor[2] = placed("factor2", [P, PACK, CHUNK], F32, PACK * PLANE_BYTES + (n_blocks + F2_HOLD) * 4 * N)
-            if k == 2:
-                nc.scalar.activation(factor[2][:, t, :], wt_wide[1][:, CHUNK:], ACT.Copy, scale=ts_slot[:, t : t + 1])
-                return
-            nc.vector.tensor_scalar(
-                factor[k][:, t, :], wt_wide[1][:, (k - 1) * CHUNK : k * CHUNK], ts_slot[:, t : t + 1], None, ALU.mult
+            nc.scalar.activation(
+                factor[:, t, h * 512 : (h + 1) * 512].rearrange("m (p c) -> m p c", c=4),
+                wt_banks[h][:].rearrange("m (c p) -> m p c", c=4),
+                ACT.Copy,
+                scale=ts_slot[:, t : t + 1],
             )
 
-        def factor_of(b):
-            k, first = (0, 0) if b < 4 else (b // 2 - 1, b // 2 * 2)
-            return factor[k][:, :, (b - first) * BLOCK : (b - first + 1) * BLOCK]
-
-        w1_in = placed("w1_in", [P, N * PACK], BF16, LAST_PLACE - 2 * N * PACK)
+        w1_in = placed("w1_in", [P, N * PACK], BF16, W1_PLACE)
+        w2_pair = sbuf("w2_pair", [P, 2 * P * PACK], BF16)
+        w2_third = sbuf("w2_third", [P, P * PACK], BF16)
+        w2_codes = sbuf("w2_codes", [P, D], U32)
         w2_scales = sbuf("w2_scales", [P, D], U8)
-        w2_in = {}
         w2_banks = {}
 
         def gather_w(j):
             nc.vector.tensor_copy(
-                w1_in[:].rearrange("p (t m j) -> p j m t", t=PACK, j=PACK)[:, j],
+                w1_in[:].rearrange("p (t q e j) -> p j q t e", t=PACK, e=RUN, j=PACK)[:, j],
                 w_planes[j][:].indirect(offsets[:]),
             )
 
@@ -157,228 +129,250 @@ def tile_attend_gnce_x_ts_kernel(tc, xT, wT, y, wt, ts, offs, out):
                 nc.tensor.transpose(turned[:, t * P : (t + 1) * P], plane[:, t], ident_bf[:])
             w2_banks[j] = turned
 
-        def group_w2(j):
-            if j == 0:
-                w2_in[0] = sbuf("w2_in0", [P, 2, P * PACK], BF16)
-            if j == 2:
-                w2_in[1] = placed("w2_in1", [P, 2, P * PACK], BF16, 0)
+        def group_w2(j, tile, first, count):
             nc.scalar.copy(
-                w2_in[j // 2][:, j % 2, :].rearrange("m (p t) -> m p t", t=PACK), w2_banks[j][:].rearrange("m (t p) -> m p t", t=PACK)
+                tile[:].rearrange("m (h j p t) -> m j h p t", h=2, j=count, t=PACK)[:, j - first],
+                w2_banks[j][:].rearrange("m (t h p) -> m h p t", t=PACK, h=2),
             )
 
-        def quantise_w2(n):
-            cols = slice(2 * n * P, 2 * (n + 1) * P)
-            nc.vector.quantize_mx(
-                w2_codes[:, cols].bitcast(E4M3), w2_scales[:, cols], w2_in[n][:].rearrange("m j c -> m (j c)")
-            )
+        def quantise_w2(tile, first, count):
+            for h in range(2):
+                cols = slice((h * PACK + first) * HALF, (h * PACK + first + count) * HALF)
+                wide = slice(h * count * HALF * PACK, (h + 1) * count * HALF * PACK)
+                nc.vector.quantize_mx(w2_codes[:, cols].bitcast(E4M3), w2_scales[:, cols], tile[:, wide])
 
+        gather_w(0)
+        turn_w(0)
         for t in range(PACK):
             make_factor(0, t)
-        for j in range(PACK):
-            if j == PACK - 1:
-                for t in range(PACK):
-                    make_factor(1, t)
-            gather_w(j)
-            turn_w(j)
-            if j < 2:
-                group_w2(j)
+        group_w2(0, w2_pair, 0, 2)
+        gather_w(1)
+        turn_w(1)
+        make_factor(1, 0)
+        group_w2(1, w2_pair, 0, 2)
+        gather_w(2)
+        turn_w(2)
+        for t in range(1, PACK):
+            make_factor(1, t)
+        group_w2(2, w2_third, 2, 1)
+        quantise_w2(w2_pair, 0, 2)
+        quantise_w2(w2_third, 2, 1)
+        gather_w(3)
+        turn_w(3)
+
 
         x_view = xT[0].rearrange("(p j) r -> p j r", j=PACK)
         x_tiles = {}
         y_tiles = {}
-        half_plane = PLANE_BYTES // 2
-        quarter_plane = PLANE_BYTES // 4
 
         def load_x(k, offset):
             x_tiles[k] = placed("x_raw%d" % k, [P, PACK, CHUNK], F32, offset)
             nc.sync.dma_start(x_tiles[k][:], x_view[:, :, k * CHUNK : (k + 1) * CHUNK])
 
-        def load_y(first, count, offset):
-            part = placed("y_raw%d" % first, [P, count, N], F32, offset)
-            rows = y[0][first * BLOCK : (first + count) * BLOCK, :]
-            nc.sync.dma_start(part[:], rows.rearrange("(c p) i -> p c i", p=P))
-            for c in range(count):
-                y_tiles[first + c] = part[:, c, :]
+        def load_y(b, offset):
+            y_tiles[b] = placed("y_raw%d" % b, [P, N], F32, offset)
+            nc.sync.dma_start(y_tiles[b][:], y[0][b * BLOCK : (b + 1) * BLOCK, :])
 
-        load_x(0, 0)
-        load_x(1, half_plane)
-        load_x(2, PLANE_BYTES)
-        load_y(0, 1, PLANE_BYTES + 2 * quarter_plane)
-        load_y(1, 1, PLANE_BYTES + 3 * quarter_plane)
-        load_y(2, 1, 2 * PLANE_BYTES)
-        load_x(3, 2 * PLANE_BYTES + quarter_plane)
-        load_y(3, 1, 2 * PLANE_BYTES + 3 * quarter_plane)
-        load_y(4, 2, LAST_PLACE + half_plane)
+        place = 0
+        for kind, k in (("x", 0), ("y", 0), ("y", 1), ("x", 1), ("y", 2), ("y", 3), ("x", 2), ("y", 4), ("y", 5), ("x", 3), ("y", 6)):
+            if kind == "x":
+                load_x(k, place)
+                place = place + 2 * TILE_BYTES
+            else:
+                load_y(k, place)
+                place = place + TILE_BYTES
 
-        units = [(0, BLOCK), (BLOCK, BLOCK), (CHUNK, CHUNK), (2 * CHUNK, CHUNK), (6 * BLOCK, BLOCK), (7 * BLOCK, BLOCK)]
+        dealt_base = W1_PLACE + 4 * TILE_BYTES
+
+        def sig_place(b):
+            return dealt_base + (b + LEAD) * 2 * TILE_BYTES
+
+        def dealt_place(b):
+            if b == 0:
+                return first_in - TILE_BYTES + 64
+            if b == 1:
+                return first_in + TILE_BYTES - 64
+            return sig_place(b - LEAD) + TILE_BYTES - 64
+
+        first_in = sig_place(n_blocks) + TILE_BYTES
+        first_codes = PACK * PLANE_BYTES - TILE_BYTES
+
         x_in = {}
         x_codes = {}
         x_scales = {}
-
-        def sig_place(b):
-            return PACK * PLANE_BYTES + (n_blocks + b) * 4 * N
-
-        def group_x(u, engine_copy):
-            first, rows = units[u]
-            k, skip = divmod(first, CHUNK)
-            if u < 4:
-                x_in[u] = placed("x_in%d" % u, [P, rows * PACK], BF16, WT_PLACE + (u == 1) * 2 * BLOCK * PACK)[:]
-            elif u >= 4:
-                x_in[u] = placed("x_in%d" % u, [P, rows * PACK], BF16, sig_place(u - X_HOLD))[:]
-            else:
-                x_in[u] = sbuf("x_in%d" % u, [P, rows * PACK], BF16)[:]
-            engine_copy(
-                x_in[u].rearrange("p (c i j) -> p c j i", i=2, j=PACK),
-                x_tiles[k][:, :, skip : skip + rows].rearrange("p j (c i) -> p c j i", i=2),
-            )
-
-        def quantise_x(u):
-            rows = units[u][1]
-            if u < 2:
-                x_codes[u] = placed("x_codes%d" % u, [P, rows], U32, W2_PLACE + 4 * D + u * 4 * BLOCK)
-            else:
-                x_codes[u] = sbuf("x_codes%d" % u, [P, rows], U32)
-            x_scales[u] = sbuf("x_scales%d" % u, [P, rows], U8)
-            nc.vector.quantize_mx(x_codes[u][:].bitcast(E4M3), x_scales[u][:], x_in[u])
-
-        w1_all = sbuf("w1_codes", [P, N], U32)
-        w1_all_scales = sbuf("w1_scales", [P, N], U8)
-        w1_codes = [w1_all[:, t * P : (t + 1) * P] for t in range(PACK)]
-        w1_scales = [w1_all_scales[:, t * P : (t + 1) * P] for t in range(PACK)]
-
-        def quantise_w1(t):
-            cols = slice(t * P, (t + 2) * P)
-            nc.vector.quantize_mx(
-                w1_all[:, cols].bitcast(E4M3), w1_all_scales[:, cols], w1_in[:, t * P * PACK : (t + 2) * P * PACK]
-            )
-
+        dealt = {}
+        y_banks = {}
         sig = {}
         diff = {}
         h_in = {}
         h_codes = {}
         h_scales = {}
+        out_banks = {}
+
+        def group_x(b, engine_copy):
+            k, skip = divmod(b * BLOCK, CHUNK)
+            if b >= LEAD + 1:
+                x_in[b] = placed("x_in%d" % b, [P, BLOCK * PACK], BF16, sig_place(b - LEAD - 1) - 64)
+            elif b == LEAD:
+                x_in[b] = placed("x_in%d" % b, [P, BLOCK * PACK], BF16, first_codes)
+            elif b == 1:
+                x_in[b] = sbuf("x_in%d" % b, [P, BLOCK * PACK], BF16)
+            else:
+                x_in[b] = placed("x_in%d" % b, [P, 2 * BLOCK * PACK], BF16, first_in)[:, 0 : BLOCK * PACK]
+            engine_copy(
+                x_in[b][:].rearrange("p (c i j) -> p c j i", i=4, j=PACK),
+                x_tiles[k][:, :, skip : skip + BLOCK].rearrange("p j (c i) -> p c j i", i=4),
+            )
+
+        def quantise_x(b):
+            if b == 1:
+                x_codes[b] = placed("x_codes%d" % b, [P, BLOCK], U32, first_in + 1024 + 64)
+            elif b >= LEAD:
+                x_codes[b] = placed("x_codes%d" % b, [P, BLOCK], U32, dealt_place(b - LEAD) + 512)
+            elif b == 0:
+                x_codes[b] = placed("x_codes%d" % b, [P, BLOCK], U32, first_codes)
+            else:
+                x_codes[b] = sbuf("x_codes%d" % b, [P, BLOCK], U32)
+            x_scales[b] = sbuf("x_scales%d" % b, [P, BLOCK], U8)
+            nc.vector.quantize_mx(x_codes[b][:].bitcast(E4M3), x_scales[b][:], x_in[b][:])
+
+        w1_codes = sbuf("w1_codes", [P, N], U32)
+        w1_scales = sbuf("w1_scales", [P, N], U8)
+
+        def quantise_w1(t):
+            cols = slice(t * P, (t + 2) * P)
+            nc.vector.quantize_mx(
+                w1_codes[:, cols].bitcast(E4M3), w1_scales[:, cols], w1_in[:, t * P * PACK : (t + 2) * P * PACK]
+            )
 
         def scores(b):
-            u = max(v for v in range(len(units)) if units[v][0] <= b * BLOCK)
-            cols = slice(b * BLOCK - units[u][0], (b + 1) * BLOCK - units[u][0])
-            sig[b] = placed("sig%d" % b, [P, PACK, BLOCK], F32, sig_place(b))
             acc = bank(b % 2)
             for t in range(PACK):
+                cols = slice(t * P, (t + 1) * P)
                 nc.tensor.matmul_mx(
-                    acc[:, t * BLOCK : (t + 1) * BLOCK],
-                    lhsT=w1_codes[t][:].bitcast(E4M3),
-                    lhsT_scale=w1_scales[t][:],
-                    rhs=x_codes[u][:, cols].bitcast(E4M3),
-                    rhs_scale=x_scales[u][:, cols],
+                    acc[:, cols],
+                    lhsT=w1_codes[:, cols].bitcast(E4M3),
+                    lhsT_scale=w1_scales[:, cols],
+                    rhs=x_codes[b][:].bitcast(E4M3),
+                    rhs_scale=x_scales[b][:],
                     start=True,
                     stop=True,
                 )
+            return acc
+
+        def sigmoid(b, acc):
+            sig[b] = placed("sig%d" % b, [P, PACK, BLOCK], F32, sig_place(b))
             for t in range(PACK):
                 nc.scalar.activation(
                     sig[b][:, t, :], acc[:, t * BLOCK : (t + 1) * BLOCK], ACT.Sigmoid, scale=ts_slot[:, t : t + 1]
                 )
 
-        def diff_place(b):
-            return PACK * PLANE_BYTES + b * 4 * N
+        def deal(b):
+            dealt[b] = placed("dealt%d" % b, [P, N], F32, dealt_place(b))
+            nc.vector.tensor_copy(
+                dealt[b][:].rearrange("r (t q e) -> r t q e", t=PACK, e=RUN),
+                y_tiles[b][:].rearrange("r (q t e) -> r t q e", t=PACK, e=RUN),
+            )
+
+        def turn_y(b):
+            y_banks[b] = bank(2 + b % 2)
+            for t in range(PACK):
+                nc.tensor.transpose(y_banks[b][:, t * P : (t + 1) * P], dealt[b][:, t * P : (t + 1) * P], ident[:])
+
+        def subtract(b):
+            diff[b] = sbuf("diff%d" % (b % 2), [P, N], F32)
+            nc.vector.tensor_tensor(diff[b][:], sig[b][:].rearrange("m t r -> m (t r)"), y_banks[b][:], ALU.subtract)
+
+        def weigh(b):
+            h_in[b] = sbuf("h_in%d" % (b % 2), [P, BLOCK * PACK], BF16)
+            nc.vector.tensor_tensor(
+                h_in[b][:].rearrange("m (c i t) -> m c t i", i=4, t=PACK),
+                diff[b][:].rearrange("m (t c i) -> m c t i", t=PACK, i=4),
+                factor[:, :, b * BLOCK : (b + 1) * BLOCK].rearrange("m t (c i) -> m c t i", i=4),
+                ALU.mult,
+            )
 
         def quantise_h(b):
-            if b + H_HOLD < n_blocks:
-                h_codes[b] = placed("h_codes%d" % b, [P, BLOCK], U32, diff_place(b + 1))
+            if b + 1 < n_blocks:
+                h_codes[b] = placed("h_codes%d" % b, [P, BLOCK], U32, dealt_place(b + 1))
             else:
                 h_codes[b] = sbuf("h_codes%d" % b, [P, BLOCK], U32)
             h_scales[b] = sbuf("h_scales%d" % b, [P, BLOCK], U8)
             nc.vector.quantize_mx(h_codes[b][:].bitcast(E5M2), h_scales[b][:], h_in[b][:])
 
-        def gradient(b, engine_copy):
-            acc = bank(OUT_BANKS[b])
+        def multiply(b, acc, cols):
             nc.tensor.matmul_mx(
-                acc[:],
+                acc,
                 lhsT=h_codes[b][:].bitcast(E5M2),
                 lhsT_scale=h_scales[b][:],
-                rhs=w2_codes[:].bitcast(E4M3),
-                rhs_scale=w2_scales[:],
+                rhs=w2_codes[:, cols].bitcast(E4M3),
+                rhs_scale=w2_scales[:, cols],
                 start=True,
                 stop=True,
             )
+
+        def gradient(b):
+            out_banks[b] = bank(4 + b % 3)
+            multiply(b, out_banks[b][:], slice(0, D))
+
+        def store(b):
             result = sbuf("result%d" % b, [P, D], F32)
-            pieces = 2 if b == n_blocks - 1 else 1
-            width = P // pieces
-            for n in range(pieces):
-                cols = slice(n * width * PACK, (n + 1) * width * PACK)
+            nc.scalar.copy(
+                result[:].rearrange("r (h p j) -> r h p j", h=2, j=PACK),
+                out_banks[b][:].rearrange("r (h j p) -> r h p j", h=2, j=PACK),
+            )
+            nc.sync.dma_start(out[0][b * BLOCK : (b + 1) * BLOCK, :], result[:])
+
+        def last_gradient(b):
+            for h, (engine_copy, queue) in enumerate(((nc.vector.tensor_copy, nc.sync), (nc.scalar.copy, nc.scalar))):
+                cols = slice(h * 256, (h + 1) * 256)
+                acc = bank(h)
+                multiply(b, acc[:, 0:256], cols)
+                result = sbuf("last%d" % h, [P, 256], F32)
                 engine_copy(
-                    result[:, cols].rearrange("r (p j) -> r p j", j=PACK),
-                    acc[:].rearrange("r (j p) -> r p j", j=PACK)[:, n * width : (n + 1) * width, :],
+                    result[:].rearrange("r (p j) -> r p j", j=PACK), acc[:, 0:256].rearrange("r (j p) -> r p j", j=PACK)
                 )
-                nc.sync.dma_start(out[0][b * BLOCK : (b + 1) * BLOCK, cols], result[:, cols])
+                queue.dma_start(out[0][b * BLOCK : (b + 1) * BLOCK, cols], result[:])
 
         group_x(0, nc.scalar.copy)
         group_x(1, nc.scalar.copy)
         quantise_w1(0)
-        quantise_x(0)
         quantise_w1(2)
+        quantise_x(0)
+        w2_last = placed("w2_last", [P, P * PACK], BF16, first_in + 64)
+        group_w2(3, w2_last, 3, 1)
+        acc = scores(0)
+        sigmoid(0, acc)
+        deal(0)
+        turn_y(0)
         quantise_x(1)
-
-        sig_banks = {}
-        diff_banks = {}
-
-        def turn_sig(b):
-            sig_banks[b] = bank(2 + b % 2)
-            for t in range(PACK):
-                nc.tensor.transpose(sig_banks[b][:, t * P : (t + 1) * P], sig[b][:, t, :], ident[:])
-
-        def subtract(b):
-            diff[b] = placed("diff%d" % b, [P, PACK, P], F32, diff_place(b))
-            nc.vector.tensor_tensor(
-                diff[b][:].rearrange("r t (c i) -> r c t i", i=2),
-                sig_banks[b][:].rearrange("r (t c i) -> r c t i", t=PACK, i=2),
-                y_tiles[b].rearrange("r (c i t) -> r c t i", t=PACK, i=2),
-                ALU.subtract,
-            )
-
-        def turn_diff(b):
-            diff_banks[b] = bank(4 + b % 2)
-            for t in range(PACK):
-                nc.tensor.transpose(diff_banks[b][:, t * P : (t + 1) * P], diff[b][:, t, :], ident[:])
-
-        def weigh(b):
-            h_in[b] = sbuf("h_in%d" % b, [P, BLOCK * PACK], BF16)
-            nc.vector.tensor_tensor(
-                h_in[b][:].rearrange("m (c i t) -> m c t i", i=2, t=PACK),
-                diff_banks[b][:].rearrange("m (t c i) -> m c t i", t=PACK, i=2),
-                factor_of(b).rearrange("m t (c i) -> m c t i", i=2),
-                ALU.mult,
-            )
-
-        group_w2(2)
-        group_w2(3)
-        scores(0)
-        scores(1)
-        w2_codes = placed("w2_codes", [P, D], U32, PLANE_BYTES // 4)
-        quantise_w2(0)
-        group_x(2, nc.vector.tensor_copy)
-        quantise_x(2)
-        group_x(3, nc.vector.tensor_copy)
-        load_y(6, 2, PLANE_BYTES)
-        quantise_w2(1)
-        quantise_x(3)
-        for s in range(-4, n_blocks + G_LAG):
-            if 0 <= s + 1 < n_blocks:
-                turn_diff(s + 1)
-            if 0 <= s + 2 < n_blocks:
-                subtract(s + 2)
-            if 0 <= s + SIG_LEAD < n_blocks:
-                turn_sig(s + SIG_LEAD)
-            if s == F2_STEP:
-                for t in range(PACK):
-                    make_factor(2, t)
-            if s in (X4_STEP, X4_STEP + 1):
-                group_x(4 + s - X4_STEP, nc.scalar.copy)
-                quantise_x(4 + s - X4_STEP)
-            if 2 <= s + SCORE_LEAD < n_blocks:
-                scores(s + SCORE_LEAD)
-            if 0 <= s < n_blocks:
-                weigh(s)
-            if 1 <= s <= n_blocks:
+        group_x(LEAD, nc.scalar.copy)
+        acc = scores(1)
+        sigmoid(1, acc)
+        deal(1)
+        turn_y(1)
+        quantise_w2(w2_last, 3, 1)
+        for s in range(n_blocks + 1):
+            if s < n_blocks:
+                subtract(s)
+            if s >= 1:
                 quantise_h(s - 1)
-            if 0 <= s - G_LAG < n_blocks:
-                gradient(s - G_LAG, nc.vector.tensor_copy if s - G_LAG == n_blocks - 1 else nc.scalar.copy)
+                if s < n_blocks:
+                    gradient(s - 1)
+                else:
+                    last_gradient(s - 1)
+            if s + LEAD < n_blocks:
+                quantise_x(s + LEAD)
+                if s == 0:
+                    load_y(n_blocks - 1, first_codes)
+                acc = scores(s + LEAD)
+                deal(s + LEAD)
+                turn_y(s + LEAD)
+            if s < n_blocks:
+                weigh(s)
+            if s + LEAD + 1 < n_blocks:
+                group_x(s + LEAD + 1, nc.scalar.copy)
+            if 1 <= s < n_blocks:
+                store(s - 1)
+            if s + LEAD < n_blocks:
+                sigmoid(s + LEAD, acc)

@@ -10,10 +10,17 @@ RUN = 8
 BLOCK = 128
 CHUNK = 256
 HALF = 64
-LEAD = 2
+SINGLE = ()
+SIG_LEAD = 3
+SCORE_LEAD = 5
+H_HOLD = 3
+OUT_BANKS = (6, 7, 6, 7, 6, 7, 0)
 PLANE_BYTES = 4 * T
 TILE_BYTES = 4 * N
-W1_PLACE = PACK * PLANE_BYTES
+LAST_PLACE = (PACK - 1) * PLANE_BYTES
+ROWS_PLACE = PACK * PLANE_BYTES
+ROWS_END = ROWS_PLACE + 16 * TILE_BYTES
+LOADS = ("x0", "x1", "x2", "y0", "y1", "y2", "x3", "y3", "y4", "y5", "y6", "y7")
 FLOPS = 2 * 2 * R * N * D
 BYTES = 4 * (D * R + D * T + R * N + R + T + R * D) + 2 * P * (N // 16)
 
@@ -58,10 +65,14 @@ def tile_attend_gnce_x_ts_kernel(tc, xT, wT, y, wt, ts, offs, out):
 
         w_view = wT.rearrange("(p j) t -> p j t", j=PACK)
         w_planes = []
-        for j in range(PACK):
+
+        def load_plane(j):
             plane = placed("plane%d" % j, [P, T], F32, j * PLANE_BYTES)
             nc.sync.dma_start(plane[:], w_view[:, j, :])
             w_planes.append(plane)
+
+        for j in range(PACK - 1):
+            load_plane(j)
 
         ident = sbuf("ident", [P, P], F32)
         make_identity(nc, ident[:])
@@ -73,7 +84,8 @@ def tile_attend_gnce_x_ts_kernel(tc, xT, wT, y, wt, ts, offs, out):
 
         factor = sbuf("factor", [P, PACK, R], F32)
         wt_banks = []
-        for h in range(2):
+
+        def spread_wt(h):
             wt_bank = bank(2 + h)
             for c in range(4):
                 col = 4 * h + c
@@ -82,18 +94,22 @@ def tile_attend_gnce_x_ts_kernel(tc, xT, wT, y, wt, ts, offs, out):
                 )
             wt_banks.append(wt_bank)
 
-        ts_listed = sbuf("ts_listed", [P, N], F32)
+        spread_wt(0)
+
+        ts_listed = placed("ts_listed", [P, (ROWS_END - LAST_PLACE) // 4], F32, LAST_PLACE)[:, 0:N]
         nc.vector.tensor_copy(
             ts_listed[:].rearrange("p (t q e) -> p q t e", t=PACK, e=RUN), ts_table[:].indirect(offsets[:])
         )
         ts_bank = bank(0)
         for t in range(PACK):
             nc.tensor.transpose(ts_bank[:, t * P : (t + 1) * P], ts_listed[:, t * P : (t + 1) * P], ident[:])
+        load_plane(PACK - 1)
+        spread_wt(1)
         ts_slot = sbuf("ts_slot", [P, PACK], F32)
         nc.scalar.copy(ts_slot[:], ts_bank[:, P - 1 :: P])
 
         def make_factor(h, t):
-            if h == 1 and t < 2:
+            if (h, t) == (0, PACK - 1):
                 nc.vector.tensor_scalar(
                     factor[:, t, h * 512 : (h + 1) * 512].rearrange("m (p c) -> m p c", c=4),
                     wt_banks[h][:].rearrange("m (c p) -> m p c", c=4),
@@ -109,7 +125,7 @@ def tile_attend_gnce_x_ts_kernel(tc, xT, wT, y, wt, ts, offs, out):
                 scale=ts_slot[:, t : t + 1],
             )
 
-        w1_in = placed("w1_in", [P, N * PACK], BF16, W1_PLACE)
+        w1_in = sbuf("w1_in", [P, N * PACK], BF16)
         w2_pair = sbuf("w2_pair", [P, 2 * P * PACK], BF16)
         w2_third = sbuf("w2_third", [P, P * PACK], BF16)
         w2_codes = sbuf("w2_codes", [P, D], U32)
@@ -143,11 +159,12 @@ def tile_attend_gnce_x_ts_kernel(tc, xT, wT, y, wt, ts, offs, out):
 
         gather_w(0)
         turn_w(0)
-        for t in range(PACK):
+        for t in range(PACK - 1):
             make_factor(0, t)
         group_w2(0, w2_pair, 0, 2)
         gather_w(1)
         turn_w(1)
+        make_factor(0, PACK - 1)
         make_factor(1, 0)
         group_w2(1, w2_pair, 0, 2)
         gather_w(2)
@@ -156,9 +173,9 @@ def tile_attend_gnce_x_ts_kernel(tc, xT, wT, y, wt, ts, offs, out):
             make_factor(1, t)
         group_w2(2, w2_third, 2, 1)
         quantise_w2(w2_pair, 0, 2)
-        quantise_w2(w2_third, 2, 1)
         gather_w(3)
         turn_w(3)
+        quantise_w2(w2_third, 2, 1)
 
 
         x_view = xT[0].rearrange("(p j) r -> p j r", j=PACK)
@@ -173,35 +190,40 @@ def tile_attend_gnce_x_ts_kernel(tc, xT, wT, y, wt, ts, offs, out):
             y_tiles[b] = placed("y_raw%d" % b, [P, N], F32, offset)
             nc.sync.dma_start(y_tiles[b][:], y[0][b * BLOCK : (b + 1) * BLOCK, :])
 
-        place = 0
-        for kind, k in (("x", 0), ("y", 0), ("y", 1), ("x", 1), ("y", 2), ("y", 3), ("x", 2), ("y", 4), ("y", 5), ("x", 3), ("y", 6)):
-            if kind == "x":
-                load_x(k, place)
+        place = ROWS_PLACE
+        for name in LOADS:
+            if name.startswith("x"):
+                load_x(int(name[1:]), place)
                 place = place + 2 * TILE_BYTES
             else:
-                load_y(k, place)
+                load_y(int(name[1:]), place)
                 place = place + TILE_BYTES
 
-        dealt_base = W1_PLACE + 4 * TILE_BYTES
+        last = n_blocks - 1
+        first_codes = LAST_PLACE
+        first_in = ROWS_END
 
         def sig_place(b):
-            return dealt_base + (b + LEAD) * 2 * TILE_BYTES
+            return first_in + (b + 1) * 2 * TILE_BYTES
 
-        def dealt_place(b):
-            if b == 0:
-                return first_in - TILE_BYTES + 64
-            if b == 1:
-                return first_in + TILE_BYTES - 64
-            return sig_place(b - LEAD) + TILE_BYTES - 64
+        def diff_place(b):
+            return sig_place(n_blocks) + b * TILE_BYTES
 
-        first_in = sig_place(n_blocks) + TILE_BYTES
-        first_codes = PACK * PLANE_BYTES - TILE_BYTES
+        def codes_place(b):
+            return diff_place(n_blocks) + b * TILE_BYTES
+
+        dealt_places = {0: ROWS_PLACE, 1: ROWS_PLACE + 2 * TILE_BYTES, last: sig_place(last - 1) + TILE_BYTES - 64}
+
+        def turned_place(b):
+            return dealt_places[b] if b in SINGLE else sig_place(b)
 
         x_in = {}
         x_codes = {}
         x_scales = {}
         dealt = {}
-        y_banks = {}
+        score_banks = {}
+        turned = {}
+        diff_banks = {}
         sig = {}
         diff = {}
         h_in = {}
@@ -209,32 +231,21 @@ def tile_attend_gnce_x_ts_kernel(tc, xT, wT, y, wt, ts, offs, out):
         h_scales = {}
         out_banks = {}
 
-        def group_x(b, engine_copy):
+        def group_x(b, count, engine_copy, tile):
             k, skip = divmod(b * BLOCK, CHUNK)
-            if b >= LEAD + 1:
-                x_in[b] = placed("x_in%d" % b, [P, BLOCK * PACK], BF16, sig_place(b - LEAD - 1) - 64)
-            elif b == LEAD:
-                x_in[b] = placed("x_in%d" % b, [P, BLOCK * PACK], BF16, first_codes)
-            elif b == 1:
-                x_in[b] = sbuf("x_in%d" % b, [P, BLOCK * PACK], BF16)
-            else:
-                x_in[b] = placed("x_in%d" % b, [P, 2 * BLOCK * PACK], BF16, first_in)[:, 0 : BLOCK * PACK]
+            x_in[b] = tile
             engine_copy(
-                x_in[b][:].rearrange("p (c i j) -> p c j i", i=4, j=PACK),
-                x_tiles[k][:, :, skip : skip + BLOCK].rearrange("p j (c i) -> p c j i", i=4),
+                tile.rearrange("p (c i j) -> p c j i", i=2, j=PACK),
+                x_tiles[k][:, :, skip : skip + count * BLOCK].rearrange("p j (c i) -> p c j i", i=2),
             )
 
-        def quantise_x(b):
-            if b == 1:
-                x_codes[b] = placed("x_codes%d" % b, [P, BLOCK], U32, first_in + 1024 + 64)
-            elif b >= LEAD:
-                x_codes[b] = placed("x_codes%d" % b, [P, BLOCK], U32, dealt_place(b - LEAD) + 512)
-            elif b == 0:
-                x_codes[b] = placed("x_codes%d" % b, [P, BLOCK], U32, first_codes)
-            else:
-                x_codes[b] = sbuf("x_codes%d" % b, [P, BLOCK], U32)
-            x_scales[b] = sbuf("x_scales%d" % b, [P, BLOCK], U8)
-            nc.vector.quantize_mx(x_codes[b][:].bitcast(E4M3), x_scales[b][:], x_in[b][:])
+        def quantise_x(b, count, offset):
+            codes = placed("x_codes%d" % b, [P, count * BLOCK], U32, offset)
+            scales = sbuf("x_scales%d" % b, [P, count * BLOCK], U8)
+            nc.vector.quantize_mx(codes[:].bitcast(E4M3), scales[:], x_in[b])
+            for c in range(count):
+                x_codes[b + c] = codes[:, c * BLOCK : (c + 1) * BLOCK]
+                x_scales[b + c] = scales[:, c * BLOCK : (c + 1) * BLOCK]
 
         w1_codes = sbuf("w1_codes", [P, N], U32)
         w1_scales = sbuf("w1_scales", [P, N], U8)
@@ -246,57 +257,73 @@ def tile_attend_gnce_x_ts_kernel(tc, xT, wT, y, wt, ts, offs, out):
             )
 
         def scores(b):
-            acc = bank(b % 2)
+            score_banks[b] = [bank(b % 2)] * PACK
+            if b == 0:
+                score_banks[b][2:] = [bank(5)] * 2
             for t in range(PACK):
                 cols = slice(t * P, (t + 1) * P)
                 nc.tensor.matmul_mx(
-                    acc[:, cols],
+                    score_banks[b][t][:, cols],
                     lhsT=w1_codes[:, cols].bitcast(E4M3),
                     lhsT_scale=w1_scales[:, cols],
-                    rhs=x_codes[b][:].bitcast(E4M3),
-                    rhs_scale=x_scales[b][:],
+                    rhs=x_codes[b].bitcast(E4M3),
+                    rhs_scale=x_scales[b],
                     start=True,
                     stop=True,
                 )
-            return acc
 
-        def sigmoid(b, acc):
-            sig[b] = placed("sig%d" % b, [P, PACK, BLOCK], F32, sig_place(b))
+        def sigmoid(b):
+            sig[b] = placed("sig%d" % b, [P, N], F32, sig_place(b))
             for t in range(PACK):
-                nc.scalar.activation(
-                    sig[b][:, t, :], acc[:, t * BLOCK : (t + 1) * BLOCK], ACT.Sigmoid, scale=ts_slot[:, t : t + 1]
-                )
+                cols = slice(t * P, (t + 1) * P)
+                nc.scalar.activation(sig[b][:, cols], score_banks[b][t][:, cols], ACT.Sigmoid, scale=ts_slot[:, t : t + 1])
 
         def deal(b):
-            dealt[b] = placed("dealt%d" % b, [P, N], F32, dealt_place(b))
+            dealt[b] = placed("dealt%d" % b, [P, N], F32, dealt_places[b])
             nc.vector.tensor_copy(
                 dealt[b][:].rearrange("r (t q e) -> r t q e", t=PACK, e=RUN),
                 y_tiles[b][:].rearrange("r (q t e) -> r t q e", t=PACK, e=RUN),
             )
 
-        def turn_y(b):
-            y_banks[b] = bank(2 + b % 2)
+        def turn(source, k):
+            target = bank(k)
             for t in range(PACK):
-                nc.tensor.transpose(y_banks[b][:, t * P : (t + 1) * P], dealt[b][:, t * P : (t + 1) * P], ident[:])
+                nc.tensor.transpose(target[:, t * P : (t + 1) * P], source[:, t * P : (t + 1) * P], ident[:])
+            return target
+
+        def turn_first(b):
+            turned[b] = turn(dealt[b] if b in SINGLE else sig[b], 2 + b % 2)
+
+        def turn_back(b):
+            diff_banks[b] = turn(diff[b], 4 + b % 2)
 
         def subtract(b):
-            diff[b] = sbuf("diff%d" % (b % 2), [P, N], F32)
-            nc.vector.tensor_tensor(diff[b][:], sig[b][:].rearrange("m t r -> m (t r)"), y_banks[b][:], ALU.subtract)
+            diff[b] = placed("diff%d" % b, [P, N], F32, diff_place(b))
+            if b in SINGLE:
+                nc.vector.tensor_tensor(diff[b][:], sig[b][:], turned[b][:], ALU.subtract)
+            else:
+                nc.vector.tensor_tensor(
+                    diff[b][:].rearrange("r (t q e) -> r q t e", t=PACK, e=RUN),
+                    turned[b][:].rearrange("r (t q e) -> r q t e", t=PACK, e=RUN),
+                    y_tiles[b][:].rearrange("r (q t e) -> r q t e", t=PACK, e=RUN),
+                    ALU.subtract,
+                )
 
         def weigh(b):
-            h_in[b] = sbuf("h_in%d" % (b % 2), [P, BLOCK * PACK], BF16)
+            h_in[b] = sbuf("h_in%d" % b, [P, BLOCK * PACK], BF16)
+            source = diff[b] if b in SINGLE else diff_banks[b]
             nc.vector.tensor_tensor(
-                h_in[b][:].rearrange("m (c i t) -> m c t i", i=4, t=PACK),
-                diff[b][:].rearrange("m (t c i) -> m c t i", t=PACK, i=4),
-                factor[:, :, b * BLOCK : (b + 1) * BLOCK].rearrange("m t (c i) -> m c t i", i=4),
+                h_in[b][:].rearrange("m (c i t) -> m c t i", i=2, t=PACK),
+                source[:].rearrange("m (t c i) -> m c t i", t=PACK, i=2),
+                factor[:, :, b * BLOCK : (b + 1) * BLOCK].rearrange("m t (c i) -> m c t i", i=2),
                 ALU.mult,
             )
 
-        def quantise_h(b):
-            if b + 1 < n_blocks:
-                h_codes[b] = placed("h_codes%d" % b, [P, BLOCK], U32, dealt_place(b + 1))
-            else:
+        def quantise_h(b, behind):
+            if behind is None:
                 h_codes[b] = sbuf("h_codes%d" % b, [P, BLOCK], U32)
+            else:
+                h_codes[b] = placed("h_codes%d" % b, [P, BLOCK], U32, diff_place(behind))
             h_scales[b] = sbuf("h_scales%d" % b, [P, BLOCK], U8)
             nc.vector.quantize_mx(h_codes[b][:].bitcast(E5M2), h_scales[b][:], h_in[b][:])
 
@@ -312,7 +339,7 @@ def tile_attend_gnce_x_ts_kernel(tc, xT, wT, y, wt, ts, offs, out):
             )
 
         def gradient(b):
-            out_banks[b] = bank(4 + b % 3)
+            out_banks[b] = bank(OUT_BANKS[b])
             multiply(b, out_banks[b][:], slice(0, D))
 
         def store(b):
@@ -326,7 +353,7 @@ def tile_attend_gnce_x_ts_kernel(tc, xT, wT, y, wt, ts, offs, out):
         def last_gradient(b):
             for h, (engine_copy, queue) in enumerate(((nc.vector.tensor_copy, nc.sync), (nc.scalar.copy, nc.scalar))):
                 cols = slice(h * 256, (h + 1) * 256)
-                acc = bank(h)
+                acc = bank(2 + h)
                 multiply(b, acc[:, 0:256], cols)
                 result = sbuf("last%d" % h, [P, 256], F32)
                 engine_copy(
@@ -334,45 +361,51 @@ def tile_attend_gnce_x_ts_kernel(tc, xT, wT, y, wt, ts, offs, out):
                 )
                 queue.dma_start(out[0][b * BLOCK : (b + 1) * BLOCK, cols], result[:])
 
-        group_x(0, nc.scalar.copy)
-        group_x(1, nc.scalar.copy)
+        def x_tile(b, count, offset):
+            return placed("x_in%d" % b, [P, count * BLOCK * PACK], BF16, offset)
+
+        def finish(b, behind):
+            quantise_h(b, behind)
+            gradient(b)
+            store(b)
+
+        def start_scores(b, offset):
+            quantise_x(b, 1, offset)
+            scores(b)
+            sigmoid(b)
+
+        group_x(0, 1, nc.scalar.copy, sbuf("x_in0", [P, BLOCK * PACK], BF16)[:])
+        group_x(1, 1, nc.scalar.copy, sbuf("x_in1", [P, BLOCK * PACK], BF16)[:])
         quantise_w1(0)
+        quantise_x(0, 1, first_codes)
         quantise_w1(2)
-        quantise_x(0)
-        w2_last = placed("w2_last", [P, P * PACK], BF16, first_in + 64)
+        w2_last = placed("w2_last", [P, P * PACK], BF16, ROWS_PLACE + TILE_BYTES)
         group_w2(3, w2_last, 3, 1)
-        acc = scores(0)
-        sigmoid(0, acc)
-        deal(0)
-        turn_y(0)
-        quantise_x(1)
-        group_x(LEAD, nc.scalar.copy)
-        acc = scores(1)
-        sigmoid(1, acc)
-        deal(1)
-        turn_y(1)
-        quantise_w2(w2_last, 3, 1)
-        for s in range(n_blocks + 1):
-            if s < n_blocks:
-                subtract(s)
-            if s >= 1:
-                quantise_h(s - 1)
-                if s < n_blocks:
-                    gradient(s - 1)
-                else:
-                    last_gradient(s - 1)
-            if s + LEAD < n_blocks:
-                quantise_x(s + LEAD)
-                if s == 0:
-                    load_y(n_blocks - 1, first_codes)
-                acc = scores(s + LEAD)
-                deal(s + LEAD)
-                turn_y(s + LEAD)
-            if s < n_blocks:
+        scores(0)
+        sigmoid(0)
+        start_scores(1, codes_place(1))
+        group_x(2, 2, nc.vector.tensor_copy, x_tile(2, 2, ROWS_PLACE)[:])
+        quantise_x(2, 2, codes_place(2))
+        group_x(4, 2, nc.vector.tensor_copy, x_tile(4, 2, ROWS_PLACE)[:])
+        quantise_x(4, 2, codes_place(4))
+        for s in range(-4, n_blocks + 1):
+            if 0 <= s + 1 < n_blocks:
+                turn_back(s + 1)
+            if 0 <= s + 2 < n_blocks:
+                subtract(s + 2)
+            if s == -1:
+                quantise_w2(w2_last, 3, 1)
+            if 0 <= s + SIG_LEAD < n_blocks:
+                turn_first(s + SIG_LEAD)
+            if s in (-1, 0):
+                group_x(7 + s, 1, nc.scalar.copy, x_tile(7 + s, 1, sig_place(3 + s))[:])
+                quantise_x(7 + s, 1, codes_place(7 + s))
+            if 2 <= s + SCORE_LEAD < n_blocks:
+                scores(s + SCORE_LEAD)
+                sigmoid(s + SCORE_LEAD)
+            if 0 <= s < n_blocks:
                 weigh(s)
-            if s + LEAD + 1 < n_blocks:
-                group_x(s + LEAD + 1, nc.scalar.copy)
-            if 1 <= s < n_blocks:
-                store(s - 1)
-            if s + LEAD < n_blocks:
-                sigmoid(s + LEAD, acc)
+            if 1 <= s <= last:
+                finish(s - 1, s if s - 1 + H_HOLD < n_blocks else None)
+        quantise_h(last, None)
+        last_gradient(last)

@@ -377,6 +377,17 @@ def tile_attend_gnce_x_ts_kernel(tc, xT, wT, y, wt, ts, offs, out):
         group_x(0, 1, nc.scalar.copy, sbuf("x_in0", [P, BLOCK * PACK], BF16)[:])
         group_x(1, 1, nc.scalar.copy, sbuf("x_in1", [P, BLOCK * PACK], BF16)[:])
         quantise_w1(0)
+        idle_bank = bank(4)
+        for n in range(2):
+            nc.tensor.matmul_mx(
+                idle_bank[:, n * 256 : (n + 1) * 256],
+                lhsT=w1_codes[:, 0:P].bitcast(E4M3),
+                lhsT_scale=w1_scales[:, 0:P],
+                rhs=w1_codes[:, 0:256].bitcast(E4M3),
+                rhs_scale=w1_scales[:, 0:256],
+                start=True,
+                stop=True,
+            )
         quantise_x(0, 1, first_codes)
         quantise_w1(2)
         w2_last = placed("w2_last", [P, P * PACK], BF16, ROWS_PLACE + TILE_BYTES)

@@ -257,9 +257,10 @@ def tile_attend_gnce_x_ts_kernel(tc, xT, wT, y, wt, ts, offs, out):
             )
 
         def scores(b):
-            score_banks[b] = [bank(b % 2)] * PACK
             if b == 0:
-                score_banks[b][2:] = [bank(5)] * 2
+                score_banks[b] = [bank(4)] * 2 + [bank(5)] * 2
+            else:
+                score_banks[b] = [bank(b % 2)] * PACK
             for t in range(PACK):
                 cols = slice(t * P, (t + 1) * P)
                 nc.tensor.matmul_mx(
@@ -377,7 +378,7 @@ def tile_attend_gnce_x_ts_kernel(tc, xT, wT, y, wt, ts, offs, out):
         group_x(0, 1, nc.scalar.copy, sbuf("x_in0", [P, BLOCK * PACK], BF16)[:])
         group_x(1, 1, nc.scalar.copy, sbuf("x_in1", [P, BLOCK * PACK], BF16)[:])
         quantise_w1(0)
-        idle_bank = bank(4)
+        idle_bank = bank(6)
         for n in range(2):
             nc.tensor.matmul_mx(
                 idle_bank[:, n * 256 : (n + 1) * 256],
@@ -395,23 +396,27 @@ def tile_attend_gnce_x_ts_kernel(tc, xT, wT, y, wt, ts, offs, out):
         scores(0)
         sigmoid(0)
         start_scores(1, codes_place(1))
-        group_x(2, 2, nc.vector.tensor_copy, x_tile(2, 2, ROWS_PLACE)[:])
-        quantise_x(2, 2, codes_place(2))
-        group_x(4, 2, nc.vector.tensor_copy, x_tile(4, 2, ROWS_PLACE)[:])
+        group_x(2, 1, nc.vector.tensor_copy, x_tile(2, 1, ROWS_PLACE)[:])
+        group_x(3, 1, nc.vector.tensor_copy, x_tile(3, 1, ROWS_PLACE + 1024)[:])
+        quantise_x(2, 1, codes_place(2))
+        quantise_x(3, 1, codes_place(3))
+        group_x(4, 2, nc.vector.tensor_copy, x_tile(4, 2, ROWS_PLACE + 2 * TILE_BYTES)[:])
+        quantise_w2(w2_last, 3, 1)
         quantise_x(4, 2, codes_place(4))
-        for s in range(-4, n_blocks + 1):
+        for s in range(-3, n_blocks + 1):
+            if s + SCORE_LEAD == 2:
+                scores(s + SCORE_LEAD)
+                sigmoid(s + SCORE_LEAD)
             if 0 <= s + 1 < n_blocks:
                 turn_back(s + 1)
             if 0 <= s + 2 < n_blocks:
                 subtract(s + 2)
-            if s == -1:
-                quantise_w2(w2_last, 3, 1)
             if 0 <= s + SIG_LEAD < n_blocks:
                 turn_first(s + SIG_LEAD)
             if s in (-1, 0):
                 group_x(7 + s, 1, nc.scalar.copy, x_tile(7 + s, 1, sig_place(3 + s))[:])
                 quantise_x(7 + s, 1, codes_place(7 + s))
-            if 2 <= s + SCORE_LEAD < n_blocks:
+            if 3 <= s + SCORE_LEAD < n_blocks:
                 scores(s + SCORE_LEAD)
                 sigmoid(s + SCORE_LEAD)
             if 0 <= s < n_blocks:

@@ -256,6 +256,19 @@ def tile_attend_gnce_x_ts_kernel(tc, xT, wT, y, wt, ts, offs, out):
                 w1_codes[:, cols].bitcast(E4M3), w1_scales[:, cols], w1_in[:, t * P * PACK : (t + 2) * P * PACK]
             )
 
+        def idle_passes(count, k):
+            target = bank(k)
+            for n in range(count):
+                nc.tensor.matmul_mx(
+                    target[:, n * 256 : (n + 1) * 256],
+                    lhsT=w1_codes[:, 0:P].bitcast(E4M3),
+                    lhsT_scale=w1_scales[:, 0:P],
+                    rhs=w1_codes[:, 0:256].bitcast(E4M3),
+                    rhs_scale=w1_scales[:, 0:256],
+                    start=True,
+                    stop=True,
+                )
+
         def scores(b):
             if b == 0:
                 score_banks[b] = [bank(4)] * 2 + [bank(5)] * 2
@@ -378,17 +391,7 @@ def tile_attend_gnce_x_ts_kernel(tc, xT, wT, y, wt, ts, offs, out):
         group_x(0, 1, nc.scalar.copy, sbuf("x_in0", [P, BLOCK * PACK], BF16)[:])
         group_x(1, 1, nc.scalar.copy, sbuf("x_in1", [P, BLOCK * PACK], BF16)[:])
         quantise_w1(0)
-        idle_bank = bank(6)
-        for n in range(2):
-            nc.tensor.matmul_mx(
-                idle_bank[:, n * 256 : (n + 1) * 256],
-                lhsT=w1_codes[:, 0:P].bitcast(E4M3),
-                lhsT_scale=w1_scales[:, 0:P],
-                rhs=w1_codes[:, 0:256].bitcast(E4M3),
-                rhs_scale=w1_scales[:, 0:256],
-                start=True,
-                stop=True,
-            )
+        idle_passes(2, 6)
         quantise_x(0, 1, first_codes)
         quantise_w1(2)
         w2_last = placed("w2_last", [P, P * PACK], BF16, ROWS_PLACE + TILE_BYTES)
@@ -413,6 +416,8 @@ def tile_attend_gnce_x_ts_kernel(tc, xT, wT, y, wt, ts, offs, out):
                 subtract(s + 2)
             if 0 <= s + SIG_LEAD < n_blocks:
                 turn_first(s + SIG_LEAD)
+            if s + SIG_LEAD == 0:
+                idle_passes(1, 5)
             if s in (-1, 0):
                 group_x(7 + s, 1, nc.scalar.copy, x_tile(7 + s, 1, sig_place(3 + s))[:])
                 quantise_x(7 + s, 1, codes_place(7 + s))

@@ -337,7 +337,7 @@ def tile_attend_gnce_x_ts_kernel(tc, xT, wT, y, wt, ts, offs, out):
             if behind is None:
                 h_codes[b] = sbuf("h_codes%d" % b, [P, BLOCK], U32)
             else:
-                h_codes[b] = placed("h_codes%d" % b, [P, BLOCK], U32, diff_place(behind))
+                h_codes[b] = placed("h_codes%d" % b, [P, BLOCK], U32, sig_place(behind) + 1024)
             h_scales[b] = sbuf("h_scales%d" % b, [P, BLOCK], U8)
             nc.vector.quantize_mx(h_codes[b][:].bitcast(E5M2), h_scales[b][:], h_in[b][:])
 
@@ -416,8 +416,6 @@ def tile_attend_gnce_x_ts_kernel(tc, xT, wT, y, wt, ts, offs, out):
                 subtract(s + 2)
             if 0 <= s + SIG_LEAD < n_blocks:
                 turn_first(s + SIG_LEAD)
-            if s + SIG_LEAD == 0:
-                idle_passes(1, 5)
             if s in (-1, 0):
                 group_x(7 + s, 1, nc.scalar.copy, x_tile(7 + s, 1, sig_place(3 + s))[:])
                 quantise_x(7 + s, 1, codes_place(7 + s))
@@ -426,7 +424,8 @@ def tile_attend_gnce_x_ts_kernel(tc, xT, wT, y, wt, ts, offs, out):
                 sigmoid(s + SCORE_LEAD)
             if 0 <= s < n_blocks:
                 weigh(s)
+                quantise_h(s, s + 2 if s + 2 < n_blocks else None)
             if 1 <= s <= last:
-                finish(s - 1, s if s - 1 + H_HOLD < n_blocks else None)
-        quantise_h(last, None)
+                gradient(s - 1)
+                store(s - 1)
         last_gradient(last)

from contextlib import ExitStack

import concourse.mybir as mybir
from concourse.masks import make_identity

N, T, D, R = 512, 2048, 512, 1024
P = 128
PACK = 4
RUN = 8
BLOCK = 128
CHUNK = 256
HALF = 64
SINGLE = ()
SIG_LEAD = 3
SCORE_LEAD = 5
H_HOLD = 3
OUT_BANKS = (6, 7, 6, 7, 6, 7, 0)
PLANE_BYTES = 4 * T
TILE_BYTES = 4 * N
LAST_PLACE = (PACK - 1) * PLANE_BYTES
ROWS_PLACE = PACK * PLANE_BYTES
ROWS_END = ROWS_PLACE + 16 * TILE_BYTES
LOADS = ("x0", "x1", "x2", "y0", "y1", "y2", "x3", "y3", "y4", "y5", "y6", "y7")
FLOPS = 2 * 2 * R * N * D
BYTES = 4 * (D * R + D * T + R * N + R + T + R * D) + 2 * P * (N // 16)

F32 = mybir.dt.float32
BF16 = mybir.dt.bfloat16
U32 = mybir.dt.uint32
U16 = mybir.dt.uint16
U8 = mybir.dt.uint8
E4M3 = mybir.dt.float8_e4m3fn_x4
E5M2 = mybir.dt.float8_e5m2_x4
ACT = mybir.ActivationFunctionType
ALU = mybir.AluOpType


def tile_attend_gnce_x_ts_kernel(tc, xT, wT, y, wt, ts, offs, out):
    nc = tc.nc
    n_blocks = R // BLOCK

    with ExitStack() as ctx:
        keep = ctx.enter_context(tc.tile_pool(name="keep", bufs=1))
        stage = ctx.enter_context(tc.tile_pool(name="stage", bufs=1))
        psum = ctx.enter_context(tc.psum_pool(name="psum", bufs=1))

        def sbuf(name, shape, dtype):
            return keep.tile(shape, dtype, name=name, align_bytes=64)

        def placed(name, shape, dtype, offset):
            return stage.tile(shape, dtype, name=name, offset=offset, align_bytes=64)

        def bank(k, dtype=F32):
            return psum.tile([P, 512], dtype, name="bank%d" % k)

        offsets = keep.tile([P, N // 16], U16, name="offsets")
        nc.sync.dma_start(offsets[:], offs)
        ts_table = sbuf("ts_table", [P, T], F32)
        nc.scalar.dma_start(ts_table[P - 1 : P, :], ts[0:1, :])
        wt_rows = sbuf("wt_rows", [P, 8], F32)
        nc.sync.dma_start(
            wt_rows[:].rearrange("p (h c) -> p h c", h=2), wt[0].rearrange("(h p c) o -> p h (c o)", h=2, c=4)
        )
        nc.vector.memset(ts_table[0 : P - 1, :], 0.0)

        w_view = wT.rearrange("(p j) t -> p j t", j=PACK)
        w_planes = []

        def load_plane(j):
            plane = placed("plane%d" % j, [P, T], F32, j * PLANE_BYTES)
            nc.sync.dma_start(plane[:], w_view[:, j, :])
            w_planes.append(plane)

        for j in range(PACK - 1):
            load_plane(j)

        ident = sbuf("ident", [P, P], F32)
        make_identity(nc, ident[:])
        ident_bf = sbuf("ident_bf", [P, P], BF16)
        make_identity(nc, ident_bf[:])

        warm = sbuf("warm", [P, 1], F32)
        nc.scalar.activation(warm[:], ident[:, 0:1], ACT.Sigmoid)

        factor = sbuf("factor", [P, PACK, R], F32)
        wt_banks = []

        def spread_wt(h):
            wt_bank = bank(2 + h)
            for c in range(4):
                col = 4 * h + c
                nc.tensor.transpose(
                    wt_bank[:, c * P : (c + 1) * P], wt_rows[:, col : col + 1].to_broadcast([P, P]), ident[:]
                )
            wt_banks.append(wt_bank)

        spread_wt(0)

        ts_listed = placed("ts_listed", [P, (ROWS_END - LAST_PLACE) // 4], F32, LAST_PLACE)[:, 0:N]
        nc.vector.tensor_copy(
            ts_listed[:].rearrange("p (t q e) -> p q t e", t=PACK, e=RUN), ts_table[:].indirect(offsets[:])
        )
        ts_bank = bank(0)
        for t in range(PACK):
            nc.tensor.transpose(ts_bank[:, t * P : (t + 1) * P], ts_listed[:, t * P : (t + 1) * P], ident[:])
        load_plane(PACK - 1)
        spread_wt(1)
        ts_slot = sbuf("ts_slot", [P, PACK], F32)
        nc.scalar.copy(ts_slot[:], ts_bank[:, P - 1 :: P])

        def make_factor(h, t):
            if (h, t) == (0, PACK - 1):
                nc.vector.tensor_scalar(
                    factor[:, t, h * 512 : (h + 1) * 512].rearrange("m (p c) -> m p c", c=4),
                    wt_banks[h][:].rearrange("m (c p) -> m p c", c=4),
                    ts_slot[:, t : t + 1],
                    None,
                    ALU.mult,
                )
                return
            nc.scalar.activation(
                factor[:, t, h * 512 : (h + 1) * 512].rearrange("m (p c) -> m p c", c=4),
                wt_banks[h][:].rearrange("m (c p) -> m p c", c=4),
                ACT.Copy,
                scale=ts_slot[:, t : t + 1],
            )

        w1_in = sbuf("w1_in", [P, N * PACK], BF16)
        w2_pair = sbuf("w2_pair", [P, 2 * P * PACK], BF16)
        w2_third = sbuf("w2_third", [P, P * PACK], BF16)
        w2_codes = sbuf("w2_codes", [P, D], U32)
        w2_scales = sbuf("w2_scales", [P, D], U8)
        w2_banks = {}

        def gather_w(j):
            nc.vector.tensor_copy(
                w1_in[:].rearrange("p (t q e j) -> p j q t e", t=PACK, e=RUN, j=PACK)[:, j],
                w_planes[j][:].indirect(offsets[:]),
            )

        def turn_w(j):
            turned = bank(6 + j % 2, BF16)
            plane = w1_in[:].rearrange("p (t m j) -> p j t m", t=PACK, j=PACK)[:, j]
            for t in range(PACK):
                nc.tensor.transpose(turned[:, t * P : (t + 1) * P], plane[:, t], ident_bf[:])
            w2_banks[j] = turned

        def group_w2(j, tile, first, count):
            nc.scalar.copy(
                tile[:].rearrange("m (h j p t) -> m j h p t", h=2, j=count, t=PACK)[:, j - first],
                w2_banks[j][:].rearrange("m (t h p) -> m h p t", t=PACK, h=2),
            )

        def quantise_w2(tile, first, count):
            for h in range(2):
                cols = slice((h * PACK + first) * HALF, (h * PACK + first + count) * HALF)
                wide = slice(h * count * HALF * PACK, (h + 1) * count * HALF * PACK)
                nc.vector.quantize_mx(w2_codes[:, cols].bitcast(E4M3), w2_scales[:, cols], tile[:, wide])

        gather_w(0)
        turn_w(0)
        for t in range(PACK - 1):
            make_factor(0, t)
        group_w2(0, w2_pair, 0, 2)
        gather_w(1)
        turn_w(1)
        make_factor(0, PACK - 1)
        make_factor(1, 0)
        group_w2(1, w2_pair, 0, 2)
        gather_w(2)
        turn_w(2)
        for t in range(1, PACK):
            make_factor(1, t)
        group_w2(2, w2_third, 2, 1)
        quantise_w2(w2_pair, 0, 2)
        gather_w(3)
        turn_w(3)
        quantise_w2(w2_third, 2, 1)


        x_view = xT[0].rearrange("(p j) r -> p j r", j=PACK)
        x_tiles = {}
        y_tiles = {}

        def load_x(k, offset):
            x_tiles[k] = placed("x_raw%d" % k, [P, PACK, CHUNK], F32, offset)
            nc.sync.dma_start(x_tiles[k][:], x_view[:, :, k * CHUNK : (k + 1) * CHUNK])

        def load_y(b, offset):
            y_tiles[b] = placed("y_raw%d" % b, [P, N], F32, offset)
            nc.sync.dma_start(y_tiles[b][:], y[0][b * BLOCK : (b + 1) * BLOCK, :])

        place = ROWS_PLACE
        for name in LOADS:
            if name.startswith("x"):
                load_x(int(name[1:]), place)
                place = place + 2 * TILE_BYTES
            else:
                load_y(int(name[1:]), place)
                place = place + TILE_BYTES

        last = n_blocks - 1
        first_codes = LAST_PLACE
        first_in = ROWS_END

        def sig_place(b):
            return first_in + (b + 1) * 2 * TILE_BYTES

        def diff_place(b):
            return sig_place(n_blocks) + b * TILE_BYTES

        def codes_place(b):
            return diff_place(n_blocks) + b * TILE_BYTES

        dealt_places = {0: ROWS_PLACE, 1: ROWS_PLACE + 2 * TILE_BYTES, last: sig_place(last - 1) + TILE_BYTES - 64}

        def turned_place(b):
            return dealt_places[b] if b in SINGLE else sig_place(b)

        x_in = {}
        x_codes = {}
        x_scales = {}
        dealt = {}
        score_banks = {}
        turned = {}
        diff_banks = {}
        sig = {}
        diff = {}
        h_in = {}
        h_codes = {}
        h_scales = {}
        out_banks = {}

        def group_x(b, count, engine_copy, tile):
            k, skip = divmod(b * BLOCK, CHUNK)
            x_in[b] = tile
            engine_copy(
                tile.rearrange("p (c i j) -> p c j i", i=2, j=PACK),
                x_tiles[k][:, :, skip : skip + count * BLOCK].rearrange("p j (c i) -> p c j i", i=2),
            )

        def quantise_x(b, count, offset):
            codes = placed("x_codes%d" % b, [P, count * BLOCK], U32, offset)
            scales = sbuf("x_scales%d" % b, [P, count * BLOCK], U8)
            nc.vector.quantize_mx(codes[:].bitcast(E4M3), scales[:], x_in[b])
            for c in range(count):
                x_codes[b + c] = codes[:, c * BLOCK : (c + 1) * BLOCK]
                x_scales[b + c] = scales[:, c * BLOCK : (c + 1) * BLOCK]

        w1_codes = sbuf("w1_codes", [P, N], U32)
        w1_scales = sbuf("w1_scales", [P, N], U8)

        def quantise_w1(t):
            cols = slice(t * P, (t + 2) * P)
            nc.vector.quantize_mx(
                w1_codes[:, cols].bitcast(E4M3), w1_scales[:, cols], w1_in[:, t * P * PACK : (t + 2) * P * PACK]
            )

        def idle_passes(count, k):
            target = bank(k)
            for n in range(count):
                nc.tensor.matmul_mx(
                    target[:, n * 256 : (n + 1) * 256],
                    lhsT=w1_codes[:, 0:P].bitcast(E4M3),
                    lhsT_scale=w1_scales[:, 0:P],
                    rhs=w1_codes[:, 0:256].bitcast(E4M3),
                    rhs_scale=w1_scales[:, 0:256],
                    start=True,
                    stop=True,
                )

        def scores(b):
            if b == 0:
                score_banks[b] = [bank(4)] * 2 + [bank(5)] * 2
            else:
                score_banks[b] = [bank(b % 2)] * PACK
            for t in range(PACK):
                cols = slice(t * P, (t + 1) * P)
                nc.tensor.matmul_mx(
                    score_banks[b][t][:, cols],
                    lhsT=w1_codes[:, cols].bitcast(E4M3),
                    lhsT_scale=w1_scales[:, cols],
                    rhs=x_codes[b].bitcast(E4M3),
                    rhs_scale=x_scales[b],
                    start=True,
                    stop=True,
                )

        def sigmoid(b):
            sig[b] = placed("sig%d" % b, [P, N], F32, sig_place(b))
            for t in range(PACK):
                cols = slice(t * P, (t + 1) * P)
                nc.scalar.activation(sig[b][:, cols], score_banks[b][t][:, cols], ACT.Sigmoid, scale=ts_slot[:, t : t + 1])

        def deal(b):
            dealt[b] = placed("dealt%d" % b, [P, N], F32, dealt_places[b])
            nc.vector.tensor_copy(
                dealt[b][:].rearrange("r (t q e) -> r t q e", t=PACK, e=RUN),
                y_tiles[b][:].rearrange("r (q t e) -> r t q e", t=PACK, e=RUN),
            )

        def turn(source, k):
            target = bank(k)
            for t in range(PACK):
                nc.tensor.transpose(target[:, t * P : (t + 1) * P], source[:, t * P : (t + 1) * P], ident[:])
            return target

        def turn_first(b):
            turned[b] = turn(dealt[b] if b in SINGLE else sig[b], 2 + b % 2)

        def turn_back(b):
            diff_banks[b] = turn(diff[b], 4 + b % 2)

        def subtract(b):
            diff[b] = placed("diff%d" % b, [P, N], F32, diff_place(b))
            if b in SINGLE:
                nc.vector.tensor_tensor(diff[b][:], sig[b][:], turned[b][:], ALU.subtract)
            else:
                nc.vector.tensor_tensor(
                    diff[b][:].rearrange("r (t q e) -> r q t e", t=PACK, e=RUN),
                    turned[b][:].rearrange("r (t q e) -> r q t e", t=PACK, e=RUN),
                    y_tiles[b][:].rearrange("r (q t e) -> r q t e", t=PACK, e=RUN),
                    ALU.subtract,
                )

        def weigh(b):
            h_in[b] = sbuf("h_in%d" % b, [P, BLOCK * PACK], BF16)
            source = diff[b] if b in SINGLE else diff_banks[b]
            nc.vector.tensor_tensor(
                h_in[b][:].rearrange("m (c i t) -> m c t i", i=2, t=PACK),
                source[:].rearrange("m (t c i) -> m c t i", t=PACK, i=2),
                factor[:, :, b * BLOCK : (b + 1) * BLOCK].rearrange("m t (c i) -> m c t i", i=2),
                ALU.mult,
            )

        def quantise_h(b, behind):
            if behind is None:
                h_codes[b] = sbuf("h_codes%d" % b, [P, BLOCK], U32)
            else:
                h_codes[b] = placed("h_codes%d" % b, [P, BLOCK], U32, sig_place(behind) + 1024)
            h_scales[b] = sbuf("h_scales%d" % b, [P, BLOCK], U8)
            nc.vector.quantize_mx(h_codes[b][:].bitcast(E5M2), h_scales[b][:], h_in[b][:])

        def multiply(b, acc, cols):
            nc.tensor.matmul_mx(
                acc,
                lhsT=h_codes[b][:].bitcast(E5M2),
                lhsT_scale=h_scales[b][:],
                rhs=w2_codes[:, cols].bitcast(E4M3),
                rhs_scale=w2_scales[:, cols],
                start=True,
                stop=True,
            )

        def gradient(b):
            out_banks[b] = bank(OUT_BANKS[b])
            multiply(b, out_banks[b][:], slice(0, D))

        def store(b):
            result = sbuf("result%d" % b, [P, D], F32)
            nc.scalar.copy(
                result[:].rearrange("r (h p j) -> r h p j", h=2, j=PACK),
                out_banks[b][:].rearrange("r (h j p) -> r h p j", h=2, j=PACK),
            )
            nc.sync.dma_start(out[0][b * BLOCK : (b + 1) * BLOCK, :], result[:])

        def last_gradient(b):
            for h, (engine_copy, queue) in enumerate(((nc.vector.tensor_copy, nc.sync), (nc.scalar.copy, nc.scalar))):
                cols = slice(h * 256, (h + 1) * 256)
                acc = bank(2 + h)
                multiply(b, acc[:, 0:256], cols)
                result = sbuf("last%d" % h, [P, 256], F32)
                engine_copy(
                    result[:].rearrange("r (p j) -> r p j", j=PACK), acc[:, 0:256].rearrange("r (j p) -> r p j", j=PACK)
                )
                queue.dma_start(out[0][b * BLOCK : (b + 1) * BLOCK, cols], result[:])

        def x_tile(b, count, offset):
            return placed("x_in%d" % b, [P, count * BLOCK * PACK], BF16, offset)

        def finish(b, behind):
            quantise_h(b, behind)
            gradient(b)
            store(b)

        def start_scores(b, offset):
            quantise_x(b, 1, offset)
            scores(b)
            sigmoid(b)

        group_x(0, 1, nc.scalar.copy, sbuf("x_in0", [P, BLOCK * PACK], BF16)[:])
        group_x(1, 1, nc.scalar.copy, sbuf("x_in1", [P, BLOCK * PACK], BF16)[:])
        quantise_w1(0)
        idle_passes(2, 6)
        quantise_x(0, 1, first_codes)
        quantise_w1(2)
        w2_last = placed("w2_last", [P, P * PACK], BF16, ROWS_PLACE + TILE_BYTES)
        group_w2(3, w2_last, 3, 1)
        scores(0)
        sigmoid(0)
        start_scores(1, codes_place(1))
        group_x(2, 1, nc.vector.tensor_copy, x_tile(2, 1, ROWS_PLACE)[:])
        group_x(3, 1, nc.vector.tensor_copy, x_tile(3, 1, ROWS_PLACE + 1024)[:])
        quantise_x(2, 1, codes_place(2))
        quantise_x(3, 1, codes_place(3))
        group_x(4, 2, nc.vector.tensor_copy, x_tile(4, 2, ROWS_PLACE + 2 * TILE_BYTES)[:])
        quantise_w2(w2_last, 3, 1)
        quantise_x(4, 2, codes_place(4))
        for s in range(-3, n_blocks + 1):
            if s + SCORE_LEAD == 2:
                scores(s + SCORE_LEAD)
                sigmoid(s + SCORE_LEAD)
            if 0 <= s + 1 < n_blocks:
                turn_back(s + 1)
            if 0 <= s + 2 < n_blocks:
                subtract(s + 2)
            if 0 <= s + SIG_LEAD < n_blocks:
                turn_first(s + SIG_LEAD)
            if s in (-1, 0):
                group_x(7 + s, 1, nc.scalar.copy, x_tile(7 + s, 1, sig_place(3 + s))[:])
                quantise_x(7 + s, 1, codes_place(7 + s))
            if 3 <= s + SCORE_LEAD < n_blocks:
                scores(s + SCORE_LEAD)
                sigmoid(s + SCORE_LEAD)
            if 0 <= s < n_blocks:
                weigh(s)
                quantise_h(s, s + 2 if s + 2 < n_blocks else None)
            if 1 <= s <= last:
                gradient(s - 1)
                store(s - 1)
        last_gradient(last)
